import numpy as np, ml_dtypes
CORES = [10,34,74,98]
N = 4
import mx_ref
BF = ml_dtypes.bfloat16
def cols(t, e):
    v = np.concatenate([t.reshape(128, -1, 4), np.zeros((128, 1, 4), BF)], axis=1)
    return np.ascontiguousarray(v[:, e]).reshape(128, -1)
def cut(t, i, w=512):
    return t[:, w * i:w * i + w]
def pick(q, e):
    c = np.concatenate([q[0].reshape(128, -1, 4), np.zeros((128, 1, 4), np.uint8)], axis=1); s = np.concatenate([q[1], np.ones((16, 1), np.uint8)], axis=1)
    return (np.ascontiguousarray(c[:, e].reshape(128, -1)), np.ascontiguousarray(s[:, e]))
def join(*qs):
    return (np.concatenate([q[0] for q in qs], axis=1), np.concatenate([q[1] for q in qs], axis=1))
def put(q, e, v):
    c, s = q[0].reshape(128, -1, 4).copy(), q[1].copy(); c[:, e] = v[0].reshape(128, -1, 4); s[:, e] = v[1]
    return (c.reshape(128, -1), s)
def pk(c, s):
    return (np.ascontiguousarray(c), mx_ref.live(s))
def emit(q):
    return q[0], q[1]
def decode(q):
    o = []
    for b in range(4):
        e = np.zeros((128, 128, 4), np.float32); e[np.arange(128), np.arange(128), b] = 1
        o.append(mx_ref.matmul(mx_ref.quantize(e.reshape(128, 512).astype(BF)), q))
    return np.stack(o, axis=2).reshape(128, -1)
def f(rng, *shape):
    return mx_ref.flush((rng.standard_normal(shape, dtype=np.float32) * np.exp2(rng.integers(-2, 3, shape[:-1] + (1,)))).astype(BF))
def wide(rng, *shape, cols=0):
    v = rng.standard_normal(shape, dtype=np.float32) * np.exp2(rng.integers(-12, 13, shape)).astype(np.float32)
    if cols: v *= np.repeat(np.exp2(rng.integers(-cols, cols + 1, shape[:-2] + (1, shape[-1] // 4))) * (rng.random(shape[:-2] + (1, shape[-1] // 4)) > 0.0625), 4, axis=-1).astype(np.float32)
    return mx_ref.flush(v.astype(BF))
M, A, E, R, O = 384, 32, 40, 3, 1
def big(v):
    v = v.astype(np.float32)
    v[np.abs(v) < np.float32(2.0 ** -14)] = 0
    return v.astype(BF)
def plain(rng):
    return {"me": big(f(rng, N, 128, 4 * M)), "x": big(f(rng, N, 128, 4 * A)), "w": f(rng, N, 128, 512 * O)}
def signs(rng, n):
    h = np.ones((1, 1))
    while len(h) < n: h = np.block([[h, h], [h, -h]])
    return h[rng.permutation(n)[:128]][:, rng.permutation(n)] * rng.choice([-1.0, 1.0], n)
def tiles(v):
    return v.reshape(-1, 128, 4).transpose(1, 0, 2).reshape(128, -1)
def store(rng, m, q):
    return {"me": big(np.stack([tiles(v) for v in m.reshape(N, M, 512)])), "x": big(np.stack([tiles(v) for v in q.reshape(N, A, 512)])), "w": f(rng, N, 128, 512 * O)}
def low(rng):
    return rng.standard_normal((N * M, 512), dtype=np.float32) * np.float32(2.0 ** -6)
def rough(rng, v):
    return v * (1 + 0.0625 * rng.uniform(-1, 1, v.shape)) * np.exp2(rng.integers(0, 2, (len(v), 1)))
def places(rng, s):
    at = np.zeros(len(s), int)
    for r in range(N):
        j = np.flatnonzero(s == r)
        at[j] = r * M + rng.permutation(M)[:len(j)]
    return at
def spare(rng, r, at):
    return rng.permutation(np.setdiff1d(np.arange(r * M, r * M + M), at))
def planted(rng, at, o):
    k, i = np.unique(at, return_inverse=True)
    v, m = signs(rng, 512), low(rng)
    m[k] = rough(rng, v[:len(k)])
    m[at[o[0]]] *= 8
    q = rough(rng, v[i])
    q[o[0]] = 4 * v[i[o[0]]] + 8 * v[i[o[-1]]]
    q[o[2]] = q[o[1]]
    return store(rng, m, q)
def setup_inputs(rng):
    return plain(rng)
def setup_inputs_hot(rng):
    h = int(rng.integers(0, N))
    g = (h + int(rng.integers(1, N))) % N
    at = (h + rng.integers(1, N, 128)) % N * M + rng.integers(0, M, 128)
    o = np.flatnonzero(np.arange(128) // A != h)
    p, u = h * M + rng.permutation(M)[:7], g * M + rng.permutation(M)[:6]
    at[o] = u[rng.integers(0, 6, len(o))]
    k = np.concatenate([o[:A], rng.permutation(o[A:-1])[:len(o) // 2 - A - 1]])
    at[k] = p[rng.integers(0, 6, len(k))]
    at[o[2]] = at[o[1]]
    at[o[-1]] = p[6]
    return planted(rng, at, o)
def setup_inputs_ties(rng):
    d, b = plain(rng), int(rng.integers(2, N))
    g = np.full((N, 4), 4.0)
    g[b] = 1
    g[(b + int(rng.integers(1, N))) % N] = 16
    p = big(np.abs(f(rng, 128, 16 * N).astype(np.float32)) * np.repeat(g.reshape(-1), 4))
    k = f(rng, 128, 120).astype(np.float32)
    k[:, :96] = np.abs(k[:, :96])
    k[:, :48] = -k[:, :48]
    k[:, :16] = k[:, :16] * np.float32(2.0 ** 24)
    k = big(k)
    e = rng.permutation(np.concatenate([np.arange(30), rng.integers(12, 24, 58), rng.integers(0, 30, 40)]))
    m = []
    for r in range(N):
        own = np.concatenate([4 * r + np.arange(4), 4 * ((r + 1) % N) + np.arange(4)])
        m.append(cols(p, rng.permutation(np.concatenate([own, own, own[rng.integers(0, 8, M - 16)]]))))
    d["me"] = np.stack(m)
    d["x"] = np.stack([cols(k, e[r * A:r * A + A]) for r in range(N)])
    return d
def setup_inputs_second(rng):
    a, b = signs(rng, 256), signs(rng, 256)
    s = rng.permutation(np.arange(128) % N)
    p = places(rng, np.concatenate([s, (s + rng.integers(1, N, 128)) % N]))
    e = rng.permutation(512)
    e, g = e[:256], e[256:]
    m, q = low(rng), rng.uniform(-1, 1, (128, 512)) * 2.0 ** -6
    q[:, e] = a
    m[p[:128, None], e] = a
    m[p[:128, None], g] = 4 * b
    m[p[128:, None], g] = 16 * b
    return store(rng, m, q)
def setup_inputs_idle(rng):
    o = rng.permutation(N)
    s = o[rng.integers(2, N, 128)]
    s[rng.permutation(128)[:E]] = o[1]
    at = places(rng, s)
    j = int(np.argmin(s))
    z = np.sort(spare(rng, int(s[j]), at)[:2])
    at[j] = z[0]
    far = spare(rng, int(s.max()), at)[0]
    v, m = signs(rng, 512), low(rng)
    v = v * v[j]
    m[at] = rough(rng, v)
    m = m - np.float32(0.25)
    m[[z[0], z[1], far]] = 0
    q = rough(rng, v)
    q[j] = 2 * q[j]
    d = store(rng, m * np.float32(2.0 ** 27), q * 2.0 ** 27)
    c = 4 * int(z[0] % M)
    d["me"][int(s[j]), :, c:c + 4] = BF(-0.0)
    return d
def setup_inputs_spread(rng):
    return {**plain(rng), "me": big(wide(rng, N, 128, 4 * M, cols=3)), "x": big(wide(rng, N, 128, 4 * A, cols=3))}
def check_inputs(d):
    b = []
    for k, least in (("me", 2.0 ** -14), ("x", 2.0 ** -14), ("w", 2.0 ** -30)):
        v = np.abs(d[k].astype(np.float32))
        if not (np.isfinite(v).all() and ((v == 0) | (v >= least) & (v <= 2.0 ** 30)).all()): b.append("a value of " + k)
    return b
def reference(me, x, w):
    mem = [mx_ref.quantize(np.ascontiguousarray(me[r])) for r in range(N)]
    q = join(*[mx_ref.quantize(np.ascontiguousarray(x[r])) for r in range(N)])
    wi = np.zeros((N, R, 128), np.float32)
    for t in range(R):
        s = np.concatenate([mx_ref.matmul(q, mem[r]) for r in range(N)], axis=1) + np.float32(0)
        win = np.argmax(s, axis=1)
        answered = np.zeros(128, bool)
        for r in range(N): answered[np.flatnonzero(win // M == r)[:E]] = True
        wi[:, t] = np.where(answered, win, -1 - win)
        half = decode(pick(join(*mem), win)) * np.float32(0.5)
        new = mx_ref.quantize((half + decode(q) * np.float32(0.5)).astype(BF))
        a = np.flatnonzero(answered)
        q = put(q, a, pick(new, a))
        for r in range(N):
            j = a[win[a] // M == r]
            if j.size:
                c, i = np.unique(win[j] - r * M, return_index=True)
                mem[r] = put(mem[r], c, pick(new, j[i]))
    oc, osc, y = np.zeros((N, 128, 4 * M), np.uint8), np.zeros((N, 16, M), np.uint8), np.zeros((N, 128, 128 * O), np.float32)
    for r in range(N):
        oc[r], osc[r] = emit(mem[r])
        for o in range(O): y[r, :, 128 * o:128 * o + 128] = mx_ref.matmul(mx_ref.quantize(np.ascontiguousarray(cut(w[r], o))), q)
    return {"oc": oc, "osc": osc, "wi": wi, "y": y}

@@ -1,0 +1,370 @@
+from concourse.bass import DstId, RemoteDMATransfer
+from concourse.mybir import dt, AluOpType, ActivationFunctionType, AxisListType
+
+M, A, E, R = 384, 32, 40, 3
+HM = M // 2
+SL = 48
+QW = 128 + 4 * SL
+FW = 14000
+CODE, U8, F32, BF, I32, U16 = "float8_e4m3fn_x4", "uint8", "float32", "bfloat16", "int32", "uint16"
+
+SCRATCH = {
+    "xt": ("sbuf", [128, 512], BF), "xq": ("sbuf", [128, 128], CODE), "xs": ("sbuf", [128, 128], U8),
+    "met": ("sbuf", [128, 4 * M], BF),
+    "wt": ("sbuf", [128, 512], BF), "wq": ("sbuf", [128, 128], CODE), "ws": ("sbuf", [128, 128], U8),
+    "ce": ("sbuf", [128, 516], F32), "et": ("sbuf", [128, 2048], BF), "eq": ("sbuf", [128, 512], CODE), "es": ("sbuf", [128, 512], U8),
+    "ints": ("sbuf", [128, 64], I32),
+    "cf": ("sbuf", [128, 1400], F32),
+    "ff": ("sbuf", [128, FW], F32),
+    "offx": ("sbuf", [128, 2], U16),
+    "places": ("sbuf", [128, 4], F32), "landp": ("sbuf", [128, 12], F32),
+    "yo": ("sbuf", [128, 128], F32),
+    "m3": ("sbuf", [128, M], CODE), "ms3": ("sbuf", [128, M], U8),
+    "q3": ("sbuf", [128, 128], CODE), "qs3": ("sbuf", [128, 128], U8),
+    "pscore": ("psum", [128, 1024], F32), "pblend": ("psum", [128, 2048], F32), "py": ("psum", [128, 512], F32),
+}
+SEMAPHORES = ["cv", "cs", "ct", "cg", "lx", "lm", "lw", "x0", "xp", "loc", "out"]
+for _t in range(R):
+    SCRATCH.update({
+        "m%d" % _t: ("sbuf", [128, 128 + M], CODE), "ms%d" % _t: ("sbuf", [128, 128 + M], U8),
+        "q%d" % _t: ("sbuf", [128, QW], CODE), "qs%d" % _t: ("sbuf", [128, QW], U8),
+        "p%d" % _t: ("sbuf", [128, 128], CODE), "ps%d" % _t: ("sbuf", [128, 128], U8),
+        "s%d" % _t: ("sbuf", [128, SL], CODE), "ss%d" % _t: ("sbuf", [128, SL], U8),
+        "h%d" % _t: ("sbuf", [128, 512], BF),
+        "land%d" % _t: ("sbuf", [128, 4], F32),
+        "oc%d" % _t: ("sbuf", [128, 8], U16), "og%d" % _t: ("sbuf", [128, 4], U16),
+        "oq%d" % _t: ("sbuf", [128, 8], U16), "om%d" % _t: ("sbuf", [128, 24], U16),
+    })
+    SEMAPHORES += ["x1_%d" % _t, "x2_%d" % _t]
+
+
+def rank_program(g, core, T, topo):
+    r = T.rank_of(core)
+    if r is None:
+        return
+    AF, OP, AXIS = ActivationFunctionType, AluOpType, AxisListType.X
+    V, S, TE = g.vector, g.scalar, g.tensor
+    others = [s for s in range(4) if s != r]
+    queue = {"v": V, "s": S, "t": TE, "g": g, "y": g.sync}
+    count = {"v": 0, "s": 0, "t": 0, "g": 0}
+    seen = {k: {} for k in queue}
+    sem = T.sem
+
+    def need(q, *deps):
+        want = {}
+        for d in deps:
+            if d is not None:
+                want[d[0]] = max(want.get(d[0], 0), d[1])
+        for n, v in want.items():
+            if seen[q].get(n, 0) < v:
+                queue[q].wait_ge(sem[n], v)
+                seen[q][n] = v
+
+    def did(q, ins):
+        count[q] += 1
+        ins.then_inc(sem["c" + q], 1)
+        return ("c" + q, count[q])
+
+    def ts(out, in0, s1, op0, s2=None, op1=None, deps=()):
+        need("v", *deps)
+        if op1 is None:
+            return did("v", V.tensor_scalar(out, in0, s1, None, op0))
+        return did("v", V.tensor_scalar(out, in0, s1, s2, op0, op1))
+
+    def tt(out, a, b, op, deps=()):
+        need("v", *deps)
+        return did("v", V.tensor_tensor(out, a, b, op))
+
+    def red(out, a, op, deps=()):
+        need("v", *deps)
+        return did("v", V.tensor_reduce(out, a, AXIS, op))
+
+    def scan(out, a, b, op0, op1, init, deps=()):
+        need("v", *deps)
+        return did("v", V.tensor_tensor_scan(out, a, b, init, op0, op1))
+
+    def tr(out, a, deps=()):
+        need("v", *deps)
+        return did("v", V.transpose(out, a))
+
+    def cp(out, a, deps=()):
+        need("v", *deps)
+        return did("v", V.tensor_copy(out, a))
+
+    def fill(ap, c):
+        return did("v", V.memset(ap, c))
+
+    def qmx(o, s, i, deps=()):
+        need("v", *deps)
+        return did("v", V.quantize_mx(o, s, i))
+
+    def act(out, a, func, deps=(), **k):
+        need("s", *deps)
+        return did("s", S.activation(out, a, func, **k))
+
+    def mm(out, l, ls, x, xs, start, stop, deps=()):
+        need("t", *deps)
+        return did("t", TE.matmul_mx(out, l, ls, x, xs, start, stop))
+
+    def io(*a, **k):
+        return did("g", g.iota(*a, **k))
+
+    used, cpos = [0], [0]
+
+    def new(n):
+        o = used[0]
+        used[0] = o + (n + 7) // 8 * 8
+        assert used[0] <= FW
+        return o
+
+    def F(o, c0, c1, p0=0, p1=128, st=1):
+        return T.ff[p0:p1, o + c0:o + c1:st]
+
+    def cnew(n):
+        o = cpos[0]
+        cpos[0] = o + (n + 7) // 8 * 8
+        return o
+
+    def C(o, c0, c1, p0=0, p1=128, st=1):
+        return T.cf[p0:p1, o + c0:o + c1:st]
+
+    local = [0]
+
+    def send(src, dsts, rsem, deps):
+        need("g", *deps)
+        mask = topo.mask(core, T.cores[others[0]])
+        ids = []
+        for s in others:
+            rid, pid, _ = topo.addr(T.cores[s])
+            mask &= topo.mask(core, T.cores[s])
+            ids.append(DstId(rid=rid, pnc=pid))
+        g.remote_dma_fused([RemoteDMATransfer(dst_ids=ids, dma_engine_mask=mask, remote_sem=sem[rsem], srcs=[src], dsts=dsts)],
+                           local_sem=sem["loc"])
+        local[0] += bin(mask).count("1")
+
+    u8, u32 = dt.uint8, dt.uint32
+    ne = len(topo.engines(core, T.cores[others[0]]))
+
+    g.sync.dma_start(T.xt[:, 0:4 * A], T.x[:, :]).then_inc(sem.lx, 16)
+    S.dma_start(T.met[:, 0:2 * M], T.me[:, 0:2 * M]).then_inc(sem.lm, 16)
+    g.sync.dma_start(T.met[:, 2 * M:4 * M], T.me[:, 2 * M:4 * M]).then_inc(sem.lm, 16)
+    g.sync.dma_start(T.wt[:, :], T.w[:, :]).then_inc(sem.lw, 16)
+
+    small = {"allow_small_or_imprecise_dtypes": True}
+    cRow, cFour = cnew(32), cnew(4)
+    i0 = io(T.ints[:, 0:1], [[0, 1]], 0, 1)
+    i1 = io(T.ints[:, 16:48], [[1, 32]], 128, -1)
+    i2 = io(C(cRow, 0, 32), [[1, 32]], 0, 0, **small)
+    i3 = io(C(cFour, 0, 4), [[1, 4]], 1, 0, **small)
+    i4 = io(T.ce[:, 512:516], [[1, 4]], 0, 4, **small)
+    i5 = io(T.ce[:, 0:512], [[1, 512]], 0, 0, **small)
+    z0 = fill(T.xt[:, 4 * A:512], 0.0)
+    cNeg, cKeep, cE, cZero, c2k = cnew(M), cnew(M), cnew(128), cnew(32), cnew(32)
+    cJ, cM16, cKb, cKc, cJ48, cPl, cNp, cP31, cB = cnew(1), cnew(1), cnew(3), cnew(1), cnew(1), cnew(3), cnew(3), cnew(1), cnew(1)
+    cMask, cTri = cnew(32), cnew(32)
+    a0 = cp(C(cJ, 0, 1), T.ints[:, 0:1], [i0])
+    b0 = ts(T.ints[:, 1:2], T.ints[:, 0:1], 15, OP.bitwise_and)
+    b1 = ts(T.ints[:, 2:3], T.ints[:, 0:1], 31, OP.bitwise_and)
+    b2 = ts(T.ints[:, 3:4], T.ints[:, 0:1], 5, OP.arith_shift_right)
+    b3 = ts(T.ints[:, 16:48], T.ints[:, 16:48], 15, OP.bitwise_and, deps=[i1])
+    a1 = cp(C(cM16, 0, 1), T.ints[:, 1:2], [b0])
+    a2 = cp(C(cP31, 0, 1), T.ints[:, 2:3], [b1])
+    a3_ = ts(C(cB, 0, 1), T.ints[:, 3:4], 64.0, OP.mult, deps=[b2])
+    for c in range(3):
+        kKb = ts(C(cKb, c, c + 1), C(cM16, 0, 1), 16.0 * c + 0.5, OP.add, deps=[a1])
+    kOx = ts(T.offx[:, 0:2], C(cKb, 0, 2), -0.5, OP.add, deps=[kKb])
+
+    qx = qmx(T.xq[:, :], T.xs[:, :], T.xt[:, :], [("lx", 16), z0])
+    o0, o1 = A * r, A * r + A
+    send(T.xq[:, 0:A].bitcast(u8), [T.q0[:, o0:o1].bitcast(u8)] * 3, "x0", [qx])
+    send(T.xs[:, 0:A], [T.qs0[:, o0:o1]] * 3, "x0", [qx])
+    own = cp(T.q0[:, o0:o1].bitcast(u32), T.xq[:, :].bitcast(u32).indirect(T.offx[:, 0:2]), [kOx, qx])
+    owns = act(T.qs0[:, o0:o1], T.xs[:, :].indirect(T.offx[:, 0:2]), AF.Copy, [kOx, qx])
+    f0 = fill(C(cNeg, 0, M), -1e29)
+    f1 = fill(C(cKeep, 0, M), 1.0)
+    memd = qmx(T.m0[:, 128:128 + M], T.ms0[:, 128:128 + M], T.met[:, :], [("lm", 32)])
+    need("v", f1)
+    f1 = fill(C(cKeep, 0, M, st=16), 0.0)
+    f2 = fill(C(cE, 0, 128), float(E))
+    f3 = fill(C(cZero, 0, 32), 0.0)
+    f4 = fill(C(c2k, 0, 32), 2048.0)
+    kmask = ts(C(cMask, 0, 32), T.ints[:, 16:48], 0.0, OP.is_equal, 1e6, OP.mult, deps=[b3])
+    kKc = ts(C(cKc, 0, 1), C(cJ, 0, 1), 2048.0, OP.add, deps=[a0])
+    kJ48 = ts(C(cJ48, 0, 1), C(cJ, 0, 1), -1.0, OP.mult, float(127 - SL), OP.add)
+    for h in range(3):
+        kPl = ts(C(cPl, h, h + 1), C(cB, 0, 1), C(cJ, 0, 1), OP.add, 128.0 + 32 * h, OP.add, deps=[a3_])
+    kTri = ts(C(cTri, 0, 32), C(cRow, 0, 32), C(cP31, 0, 1), OP.is_ge, 1e6, OP.mult, deps=[a2, i2])
+    kNp = ts(C(cNp, 0, 3), C(cPl, 0, 3), -127.0, OP.add, -2048.0, OP.mult, deps=[kPl])
+    for b in range(4):
+        ke = ts(T.et[:, 512 * b:512 * b + 512], T.ce[:, 0:512], T.ce[:, 512 + b:513 + b], OP.is_equal, 0.5, OP.mult, deps=[i4, i5])
+    ke = qmx(T.eq[:, :], T.es[:, :], T.et[:, :], [ke])
+    WR, OH, A3 = new(128), new(12), new(3)
+    fWR = fill(F(WR, 0, 128), 0.0)
+    RWs, CSs = [new(5) for _ in range(R)], [new(136) for _ in range(R)]
+    for t in range(R):
+        fRW = fill(F(RWs[t], 0, 1), -1e29)
+        fRW = fill(F(CSs[t], 0, 8), 0.0)
+    kw = qmx(T.wq[:, :], T.ws[:, :], T.wt[:, :], [("lw", 16)])
+
+    qdeps = [own, owns, ("x0", 2 * ne * 3)]
+    mdeps = [memd]
+    scan_prev, cast_prev = [None, None], []
+    for t in range(R):
+        land = T["land%d" % t]
+        m, ms, q, qs = T["m%d" % t], T["ms%d" % t], T["q%d" % t], T["qs%d" % t]
+        p, ps, s_, ss_ = T["p%d" % t], T["ps%d" % t], T["s%d" % t], T["ss%d" % t]
+        h = T["h%d" % t]
+        oc, og, oq, om = T["oc%d" % t], T["og%d" % t], T["oq%d" % t], T["om%d" % t]
+        RM, JK, CN = new(M), new(M), new(1)
+        sc = []
+        for k in range(2):
+            sc.append(mm(T.pscore[:, 512 * k:512 * k + HM], q[:, 0:128], qs[:, 0:128], m[:, 128 + HM * k:128 + HM * k + HM],
+                         ms[:, 128 + HM * k:128 + HM * k + HM], True, True, qdeps + mdeps + [scan_prev[k]]))
+        rm = scan(F(RM, 0, HM), T.pscore[:, 0:HM], C(cNeg, 0, HM), OP.max, OP.max, -1e29, [sc[0], f0])
+        rm2 = scan(F(RM, HM, M), T.pscore[:, 512:512 + HM], C(cNeg, 0, HM), OP.max, OP.max, F(RM, HM - 1, HM), [sc[1], rm])
+        scan_prev, rm = [rm, rm2], rm2
+        send(F(RM, M - 1, M), [land[:, r:r + 1]] * 3, "x1_%d" % t, [rm])
+        for b in range(4):
+            dq = mm(T.pblend[:, 512 * b:512 * b + 128], T.eq[:, 128 * b:128 * b + 128], T.es[:, 128 * b:128 * b + 128],
+                    q[:, 0:128], qs[:, 0:128], True, False, [ke] + cast_prev)
+        cn = act(F(JK, 0, M), F(RM, 0, M), AF.Sign, [rm], scale=-1.0, bias=F(RM, M - 1, M), accum_out=F(CN, 0, 1))
+        B1, R1, R2 = new(32), new(128), new(128)
+        bc = ts(F(B1, 0, 32), C(cMask, 0, 32), F(CN, 0, 1), OP.min, deps=[cn, kmask])
+        for a in range(4):
+            x = tr(F(R1, 32 * a, 32 * a + 32, 0, 32), F(B1, 0, 32, 32 * a, 32 * a + 32), [bc])
+        x = scan(F(R2, 0, 128, 0, 32), C(cKeep, 0, 128, 0, 32), F(R1, 0, 128, 0, 32), OP.mult, OP.add, 0.0, [x, f1])
+        for a in range(4):
+            lc = cp(oc[32 * a:32 * a + 32, 0:8], F(R2, 15, 128, 0, 32, 16), [x])
+        OW, KB, KF = new(32), new(32), new(128)
+        ow = act(F(OW, 0, 32), C(cZero, 0, 32), AF.Identity, [f3], bias=F(RM, M - 1, M))
+        kb = act(F(KB, 0, 32), C(c2k, 0, 32), AF.Identity, [f4, cn, kKc], scale=F(CN, 0, 1), bias=C(cKc, 0, 1))
+        pl = act(T.places[:, t:t + 1], F(CN, 0, 1), AF.Copy, [cn], bias=float(M * r))
+        if t == R - 1:
+            send(T.places[:, 0:R], [T.landp[:, R * r:R * r + R]] * 3, "xp", [pl])
+        pkc = cp(p[:, :].bitcast(u32), m[:, 128:128 + M].bitcast(u32).indirect(oc[:, 0:8]), [lc] + mdeps)
+        pks = act(ps[:, :], ms[:, 128:128 + M].indirect(oc[:, 0:8]), AF.Copy, [lc] + mdeps)
+        for a in range(4):
+            kf = tr(F(KF, 32 * a, 32 * a + 32, 0, 32), F(KB, 0, 32, 32 * a, 32 * a + 32), [kb])
+        bl = []
+        for b in range(4):
+            bl.append(mm(T.pblend[:, 512 * b:512 * b + 128], T.eq[:, 128 * b:128 * b + 128], T.es[:, 128 * b:128 * b + 128],
+                         p[:, :], ps[:, :], False, True, [pkc, pks]))
+        cast_prev = []
+        for b in (0, 2):
+            cast_prev.append(cp(h[:, b:512:4], T.pblend[:, 512 * b:512 * b + 128], [bl[b]]))
+            cast_prev.append(act(h[:, b + 1:512:4], T.pblend[:, 512 * b + 512:512 * b + 640], AF.Copy, [bl[b + 1]]))
+        nd = qmx(m[:, 0:128], ms[:, 0:128], h[:, :], cast_prev)
+        x1 = ("x1_%d" % t, 3 * ne)
+        MX, FL, MI, MR, AC, AN, KR = new(1), new(1), new(32), new(128), new(3), new(128), new(128)
+        col = [land[:, s:s + 1] for s in range(4)]
+        me = F(RM, M - 1, M)
+        if r == 0:
+            x = red(F(MX, 0, 1), land[:, 1:4], OP.max, [x1])
+            mi = ts(F(MI, 0, 32), F(OW, 0, 32), F(MX, 0, 1), OP.is_ge, deps=[x, ow])
+        elif r == 3:
+            x = red(F(MX, 0, 1), land[:, 0:3], OP.max, [x1])
+            mi = ts(F(MI, 0, 32), F(OW, 0, 32), F(MX, 0, 1), OP.is_gt, deps=[x, ow])
+        elif r == 1:
+            x = tt(F(MX, 0, 1), col[2], col[3], OP.max, [x1])
+            x = ts(F(FL, 0, 1), me, col[0], OP.is_gt)
+            mi = ts(F(MI, 0, 32), F(OW, 0, 32), F(MX, 0, 1), OP.is_ge, F(FL, 0, 1), OP.mult, deps=[x, ow])
+        else:
+            x = tt(F(MX, 0, 1), col[0], col[1], OP.max, [x1])
+            x = ts(F(FL, 0, 1), me, col[3], OP.is_ge)
+            mi = ts(F(MI, 0, 32), F(OW, 0, 32), F(MX, 0, 1), OP.is_gt, F(FL, 0, 1), OP.mult, deps=[x, ow])
+        lo = act(land[:, r:r + 1], me, AF.Copy, [x1])
+        for a in range(4):
+            x = tr(F(MR, 32 * a, 32 * a + 32, 0, 32), F(MI, 0, 32, 32 * a, 32 * a + 32), [mi])
+        CS = CSs[t]
+        cs = scan(F(CS, 8, 136, 0, 32), F(MR, 0, 128, 0, 32), C(cE, 0, 128, 0, 32), OP.add, OP.min, 0.0, [x, f2])
+        for c in range(3):
+            ac = act(F(new(128), 0, 128, 0, 32), F(CS, 8, 136, 0, 32), AF.Sign, [cs, kKb], scale=-1.0, bias=C(cKb, c, c + 1, 0, 32),
+                     accum_out=F(AC, c, c + 1, 0, 32))
+        an = tt(F(AN, 0, 128, 0, 32), F(CS, 8, 136, 0, 32), F(CS, 7, 135, 0, 32), OP.subtract, [cs, fRW])
+        RW, S1, TC = RWs[t], new(1), new(1)
+        rw = scan(F(RW, 1, 5), land[:, 0:4], C(cNeg, 0, 4), OP.max, OP.max, -1e29, [lo, x1])
+        kr = tt(F(KR, 0, 128, 0, 32), F(AN, 0, 128, 0, 32), F(KF, 0, 128, 0, 32), OP.mult, [an, kf])
+        for a in range(4):
+            lg = ts(og[32 * a:32 * a + 32, 0:3], F(AC, 0, 3, 0, 32), 0.5, OP.mult, 64.0, OP.add, deps=[ac])
+        gc = cp(s_[:, :].bitcast(u32), m[:, :].bitcast(u32).indirect(og[:, 0:3]), [lg, nd])
+        gs = act(ss_[:, :], ms[:, :].indirect(og[:, 0:3]), AF.Copy, [lg, nd])
+        k0 = 128 + SL * r
+        x2 = "x2_%d" % t
+        send(s_[:, 0:E].bitcast(u8), [q[:, k0:k0 + E].bitcast(u8)] * 3, x2, [gc])
+        send(ss_[:, 0:E], [qs[:, k0:k0 + E]] * 3, x2, [gs])
+        J3, BW, BT, EQ, P, Z, L = new(5), new(32), new(32), new(128), new(1), new(1), new(1)
+        s1 = act(F(J3, 0, 5), F(RW, 0, 5), AF.Sign, [rw], scale=-1.0, bias=F(RW, 4, 5), accum_out=F(S1, 0, 1))
+        bw = act(F(BW, 0, 32), C(cZero, 0, 32), AF.Identity, [s1], bias=F(S1, 0, 1))
+        tc = act(F(TC, 0, 1), F(S1, 0, 1), AF.Identity, [kJ48], scale=float(SL), bias=C(cJ48, 0, 1))
+        for b in (1, 2, 3):
+            kk = act(F(KR, 0, 128, 32 * b, 32 * b + 32), F(KR, 0, 128, 0, 32), AF.Copy, [kr])
+        AB = new(M)
+        ab = []
+        for c in range(3):
+            ab.append(act(F(AB, 128 * c, 128 * c + 128), F(KR, 0, 128), AF.Abs, [kk, kNp], bias=C(cNp, c, c + 1)))
+        bt = ts(F(BT, 0, 32), C(cTri, 0, 32), F(S1, 0, 1), OP.min, deps=[s1, kTri])
+        for b in range(1, 4):
+            for a in range(b):
+                x = tr(F(WR, 32 + 32 * a, 64 + 32 * a, 32 * b, 32 * b + 32), F(BW, 0, 32, 32 * a, 32 * a + 32), [bw, fWR])
+        x = tr(F(WR, 0, 32), F(BT, 0, 32), [bt])
+        x = ts(F(EQ, 0, 128), F(WR, 0, 128), F(S1, 0, 1), OP.is_equal, deps=[x])
+        x = red(F(P, 0, 1), F(EQ, 0, 128), OP.add, [x])
+        z = ts(F(A3, t, t + 1), F(P, 0, 1), float(E), OP.is_le, deps=[x])
+        z = tt(F(Z, 0, 1), F(P, 0, 1), F(TC, 0, 1), OP.add, [tc])
+        z = ts(F(L, 0, 1), F(Z, 0, 1), F(A3, t, t + 1), OP.mult, C(cJ, 0, 1), OP.add, deps=[z])
+        B2, R3, R4 = new(32), new(128), new(128)
+        z = ts(F(B2, 0, 32), C(cMask, 0, 32), F(L, 0, 1), OP.min, deps=[z])
+        for a in range(4):
+            x = tr(F(R3, 32 * a, 32 * a + 32, 0, 32), F(B2, 0, 32, 32 * a, 32 * a + 32), [z])
+        x = scan(F(R4, 0, 128, 0, 32), C(cKeep, 0, 128, 0, 32), F(R3, 0, 128, 0, 32), OP.mult, OP.add, 0.0, [x])
+        for a in range(4):
+            lq = cp(oq[32 * a:32 * a + 32, 0:8], F(R4, 15, 128, 0, 32, 16), [x])
+        D, BM, R5, R6 = new(3), new(96), new(M), new(M)
+        for c in range(3):
+            d = red(F(D, c, c + 1), F(AB, 128 * c, 128 * c + 128), OP.min, [ab[c]])
+        for c in range(3):
+            x = ts(F(BM, 32 * c, 32 * c + 32), C(cMask, 0, 32), F(D, c, c + 1), OP.min, C(cPl, c, c + 1), OP.min, deps=[("cv", d[1] - 2 + c)])
+        for a in range(4):
+            y = tr(F(R5, 96 * a, 96 * a + 96, 0, 32), F(BM, 0, 96, 32 * a, 32 * a + 32), [x])
+        x = scan(F(R6, 0, M, 0, 32), C(cKeep, 0, M, 0, 32), F(R5, 0, M, 0, 32), OP.mult, OP.add, 0.0, [y])
+        for a in range(4):
+            lm = cp(om[32 * a:32 * a + 32, 0:24], F(R6, 15, M, 0, 32, 16), [x])
+        oh = ts(F(OH, t, 12, st=3), C(cFour, 0, 4), F(S1, 0, 1), OP.is_equal, deps=[i3])
+        gc = cp(q[:, k0:k0 + SL].bitcast(u32), m[:, :].bitcast(u32).indirect(og[:, 0:3]))
+        gs = act(qs[:, k0:k0 + SL], ms[:, :].indirect(og[:, 0:3]), AF.Copy)
+        if t < R - 1:
+            m2, ms2, c0 = T["m%d" % (t + 1)], T["ms%d" % (t + 1)], 128
+        else:
+            m2, ms2, c0 = T.m3, T.ms3, 0
+        mc = cp(m2[:, c0:c0 + M].bitcast(u32), m[:, :].bitcast(u32).indirect(om[:, 0:24]), [lm, nd] + mdeps)
+        mp = act(ms2[:, c0:c0 + M], ms[:, :].indirect(om[:, 0:24]), AF.Copy, [lm, nd] + mdeps)
+        mdeps = [mc, mp]
+        if t == R - 1:
+            need("y", mc, mp)
+            g.sync.dma_start(T.oc[:, :], T.m3[:, :].bitcast(u8)).then_inc(sem.out, 16)
+            for k in range(4):
+                g.sync.dma_start(T.osc[4 * k:4 * k + 4, :], T.ms3[32 * k:32 * k + 4, :]).then_inc(sem.out, 16)
+            xp = ("xp", 3 * ne)
+            lp = act(T.landp[:, R * r:R * r + R], T.places[:, 0:R], AF.Copy, [xp, pl])
+            G12, G3, SG, AM, W1, WO = new(12), new(3), new(3), new(3), new(3), new(3)
+            sg = ts(F(SG, 0, 3), F(A3, 0, 3), 2.0, OP.mult, -1.0, OP.add)
+            sg = ts(F(AM, 0, 3), F(A3, 0, 3), -1.0, OP.add)
+            x = tt(F(G12, 0, 12), F(OH, 0, 12), T.landp[:, :], OP.mult, [oh, lp, xp])
+            for c in range(3):
+                x2_ = red(F(G3, c, c + 1), F(G12, c, 12, st=3), OP.add, [x])
+            x = tt(F(W1, 0, 3), F(G3, 0, 3), F(SG, 0, 3), OP.mult, [x2_])
+            x = tt(F(WO, 0, 3), F(W1, 0, 3), F(AM, 0, 3), OP.add, [x])
+            need("y", x)
+            for c in range(R):
+                g.sync.dma_start(T.wi[c:c + 1, :], F(WO, c, c + 1)).then_inc(sem.out, 16)
+        q2, qs2 = T["q%d" % (t + 1)], T["qs%d" % (t + 1)]
+        xx = (x2, 2 * 3 * ne)
+        a = cp(q2[:, 0:128].bitcast(u32), q[:, :].bitcast(u32).indirect(oq[:, 0:8]), [lq, gc, xx] + qdeps)
+        b = act(qs2[:, 0:128], qs[:, :].indirect(oq[:, 0:8]), AF.Copy, [lq, gs, xx] + qdeps)
+        qdeps = [a, b]
+    y = mm(T.py[:, 0:128], T.wq[:, :], T.ws[:, :], T.q3[:, :], T.qs3[:, :], True, True, [kw] + qdeps)
+    y = cp(T.yo[:, :], T.py[:, 0:128], [y])
+    need("y", y)
+    g.sync.dma_start(T.y[:, :], T.yo[:, :]).then_inc(sem.out, 16)
+    need("y", ("out", 16 * (1 + 4 + R + 1)))
+    need("g", ("loc", local[0]), *[("c" + k, n) for k, n in count.items()])

@@ -12,9 +12,9 @@ SCRATCH = {
     "xt": ("sbuf", [128, 512], BF), "xq": ("sbuf", [128, 128], CODE), "xs": ("sbuf", [128, 128], U8),
     "met": ("sbuf", [128, 4 * M], BF),
     "wt": ("sbuf", [128, 512], BF), "wq": ("sbuf", [128, 128], CODE), "ws": ("sbuf", [128, 128], U8),
-    "ce": ("sbuf", [128, 516], F32), "et": ("sbuf", [128, 2048], BF), "eq": ("sbuf", [128, 512], CODE), "es": ("sbuf", [128, 512], U8),
+    "ce": ("sbuf", [128, 520 + 1024], F32), "et": ("sbuf", [128, 2048], BF), "eq": ("sbuf", [128, 512], CODE), "es": ("sbuf", [128, 512], U8),
     "ints": ("sbuf", [128, 64], I32),
-    "cf": ("sbuf", [128, 1400], F32),
+    "cf": ("sbuf", [128, 1000], F32),
     "ff": ("sbuf", [128, FW], F32),
     "offx": ("sbuf", [128, 2], U16),
     "places": ("sbuf", [128, 4], F32), "landp": ("sbuf", [128, 12], F32),
@@ -35,7 +35,7 @@ for _t in range(R):
         "oc%d" % _t: ("sbuf", [128, 8], U16), "og%d" % _t: ("sbuf", [128, 4], U16),
         "oq%d" % _t: ("sbuf", [128, 8], U16), "om%d" % _t: ("sbuf", [128, 24], U16),
     })
-    SEMAPHORES += ["x1_%d" % _t, "x2_%d" % _t]
+    SEMAPHORES += ["x1_%d" % _t, "x2_%d" % _t, "own%d" % _t]
 
 
 def rank_program(g, core, T, topo):
@@ -44,7 +44,7 @@ def rank_program(g, core, T, topo):
         return
     AF, OP, AXIS = ActivationFunctionType, AluOpType, AxisListType.X
     V, S, TE = g.vector, g.scalar, g.tensor
-    others = [s for s in range(4) if s != r]
+    others = [(r + k) % 4 for k in (1, 2, 3)]
     queue = {"v": V, "s": S, "t": TE, "g": g, "y": g.sync}
     count = {"v": 0, "s": 0, "t": 0, "g": 0}
     seen = {k: {} for k in queue}
@@ -159,8 +159,8 @@ def rank_program(g, core, T, topo):
     i4 = io(T.ce[:, 512:516], [[1, 4]], 0, 4, **small)
     i5 = io(T.ce[:, 0:512], [[1, 512]], 0, 0, **small)
     z0 = fill(T.xt[:, 4 * A:512], 0.0)
-    cNeg, cKeep, cE, cZero, c2k = cnew(M), cnew(M), cnew(128), cnew(32), cnew(32)
-    cJ, cM16, cKb, cKc, cJ48, cPl, cNp, cP31, cB = cnew(1), cnew(1), cnew(3), cnew(1), cnew(1), cnew(3), cnew(3), cnew(1), cnew(1)
+    cNeg, cKeep, cE, cZero, c2k = cnew(HM), cnew(128), cnew(128), cnew(32), cnew(32)
+    cJ, cM16, cKb, cKc, cT0, cT1, cPl, cNp, cP31, cB = [cnew(n) for n in (1, 1, 3, 1, 1, 1, 3, 3, 1, 1)]
     cMask, cTri = cnew(32), cnew(32)
     a0 = cp(C(cJ, 0, 1), T.ints[:, 0:1], [i0])
     b0 = ts(T.ints[:, 1:2], T.ints[:, 0:1], 15, OP.bitwise_and)
@@ -180,30 +180,33 @@ def rank_program(g, core, T, topo):
     send(T.xs[:, 0:A], [T.qs0[:, o0:o1]] * 3, "x0", [qx])
     own = cp(T.q0[:, o0:o1].bitcast(u32), T.xq[:, :].bitcast(u32).indirect(T.offx[:, 0:2]), [kOx, qx])
     owns = act(T.qs0[:, o0:o1], T.xs[:, :].indirect(T.offx[:, 0:2]), AF.Copy, [kOx, qx])
-    f0 = fill(C(cNeg, 0, M), -1e29)
-    f1 = fill(C(cKeep, 0, M), 1.0)
-    memd = qmx(T.m0[:, 128:128 + M], T.ms0[:, 128:128 + M], T.met[:, :], [("lm", 32)])
-    need("v", f1)
-    f1 = fill(C(cKeep, 0, M, st=16), 0.0)
+    ke = []
+    for b in range(2):
+        x = act(T.ce[:, 520 + 512 * b:1032 + 512 * b], T.ce[:, 0:512], AF.Abs, [i4, i5], scale=-1.0, bias=T.ce[:, 512 + b:513 + b])
+        ke.append(act(T.et[:, 512 * b:512 * b + 512], T.ce[:, 520 + 512 * b:1032 + 512 * b], AF.Relu, [x], scale=-1.0, bias=0.5))
+    f0 = fill(C(cNeg, 0, HM), -1e29)
+    f1 = fill(C(cKeep, 0, 128), 1.0)
     f2 = fill(C(cE, 0, 128), float(E))
     f3 = fill(C(cZero, 0, 32), 0.0)
+    memd = qmx(T.m0[:, 128:128 + M], T.ms0[:, 128:128 + M], T.met[:, :], [("lm", 32)])
     f4 = fill(C(c2k, 0, 32), 2048.0)
+    need("v", f1)
+    f1 = fill(C(cKeep, 0, 128, st=16), 0.0)
+    for b in (2, 3):
+        ke.append(ts(T.et[:, 512 * b:512 * b + 512], T.ce[:, 0:512], T.ce[:, 512 + b:513 + b], OP.is_equal, 0.5, OP.mult, deps=[i4, i5]))
     kmask = ts(C(cMask, 0, 32), T.ints[:, 16:48], 0.0, OP.is_equal, 1e6, OP.mult, deps=[b3])
     kKc = ts(C(cKc, 0, 1), C(cJ, 0, 1), 2048.0, OP.add, deps=[a0])
-    kJ48 = ts(C(cJ48, 0, 1), C(cJ, 0, 1), -1.0, OP.mult, float(127 - SL), OP.add)
+    kT = ts(C(cT0, 0, 1), C(cJ, 0, 1), -1.0, OP.mult, float(127 - SL), OP.add)
+    kT = ts(C(cT1, 0, 1), C(cJ, 0, 1), -1.0, OP.mult, float(127 - SL + E), OP.add)
     for h in range(3):
         kPl = ts(C(cPl, h, h + 1), C(cB, 0, 1), C(cJ, 0, 1), OP.add, 128.0 + 32 * h, OP.add, deps=[a3_])
     kTri = ts(C(cTri, 0, 32), C(cRow, 0, 32), C(cP31, 0, 1), OP.is_ge, 1e6, OP.mult, deps=[a2, i2])
     kNp = ts(C(cNp, 0, 3), C(cPl, 0, 3), -127.0, OP.add, -2048.0, OP.mult, deps=[kPl])
-    for b in range(4):
-        ke = ts(T.et[:, 512 * b:512 * b + 512], T.ce[:, 0:512], T.ce[:, 512 + b:513 + b], OP.is_equal, 0.5, OP.mult, deps=[i4, i5])
-    ke = qmx(T.eq[:, :], T.es[:, :], T.et[:, :], [ke])
-    WR, OH, A3 = new(128), new(12), new(3)
+    ke = qmx(T.eq[:, :], T.es[:, :], T.et[:, :], ke)
+    WR, OH, A3, KF, RW3 = new(128), new(12), new(3), new(136), new(8 * R)
     fWR = fill(F(WR, 0, 128), 0.0)
-    RWs, CSs = [new(5) for _ in range(R)], [new(136) for _ in range(R)]
-    for t in range(R):
-        fRW = fill(F(RWs[t], 0, 1), -1e29)
-        fRW = fill(F(CSs[t], 0, 8), 0.0)
+    fKF = fill(F(KF, 128, 136), 0.0)
+    fRW = fill(F(RW3, 0, 8 * R), -1e29)
     kw = qmx(T.wq[:, :], T.ws[:, :], T.wt[:, :], [("lw", 16)])
 
     qdeps = [own, owns, ("x0", 2 * ne * 3)]
@@ -215,7 +218,9 @@ def rank_program(g, core, T, topo):
         p, ps, s_, ss_ = T["p%d" % t], T["ps%d" % t], T["s%d" % t], T["ss%d" % t]
         h = T["h%d" % t]
         oc, og, oq, om = T["oc%d" % t], T["og%d" % t], T["oq%d" % t], T["om%d" % t]
+        last = t == R - 1
         RM, JK, CN = new(M), new(M), new(1)
+        me = F(RM, M - 1, M)
         sc = []
         for k in range(2):
             sc.append(mm(T.pscore[:, 512 * k:512 * k + HM], q[:, 0:128], qs[:, 0:128], m[:, 128 + HM * k:128 + HM * k + HM],
@@ -223,11 +228,11 @@ def rank_program(g, core, T, topo):
         rm = scan(F(RM, 0, HM), T.pscore[:, 0:HM], C(cNeg, 0, HM), OP.max, OP.max, -1e29, [sc[0], f0])
         rm2 = scan(F(RM, HM, M), T.pscore[:, 512:512 + HM], C(cNeg, 0, HM), OP.max, OP.max, F(RM, HM - 1, HM), [sc[1], rm])
         scan_prev, rm = [rm, rm2], rm2
-        send(F(RM, M - 1, M), [land[:, r:r + 1]] * 3, "x1_%d" % t, [rm])
+        send(me, [land[:, r:r + 1]] * 3, "x1_%d" % t, [rm])
         for b in range(4):
             dq = mm(T.pblend[:, 512 * b:512 * b + 128], T.eq[:, 128 * b:128 * b + 128], T.es[:, 128 * b:128 * b + 128],
                     q[:, 0:128], qs[:, 0:128], True, False, [ke] + cast_prev)
-        cn = act(F(JK, 0, M), F(RM, 0, M), AF.Sign, [rm], scale=-1.0, bias=F(RM, M - 1, M), accum_out=F(CN, 0, 1))
+        cn = act(F(JK, 0, M), F(RM, 0, M), AF.Sign, [rm], scale=-1.0, bias=me, accum_out=F(CN, 0, 1))
         B1, R1, R2 = new(32), new(128), new(128)
         bc = ts(F(B1, 0, 32), C(cMask, 0, 32), F(CN, 0, 1), OP.min, deps=[cn, kmask])
         for a in range(4):
@@ -235,11 +240,11 @@ def rank_program(g, core, T, topo):
         x = scan(F(R2, 0, 128, 0, 32), C(cKeep, 0, 128, 0, 32), F(R1, 0, 128, 0, 32), OP.mult, OP.add, 0.0, [x, f1])
         for a in range(4):
             lc = cp(oc[32 * a:32 * a + 32, 0:8], F(R2, 15, 128, 0, 32, 16), [x])
-        OW, KB, KF = new(32), new(32), new(128)
-        ow = act(F(OW, 0, 32), C(cZero, 0, 32), AF.Identity, [f3], bias=F(RM, M - 1, M))
+        OW, KB = new(32), new(32)
+        ow = act(F(OW, 0, 32), C(cZero, 0, 32), AF.Identity, [f3], bias=me)
         kb = act(F(KB, 0, 32), C(c2k, 0, 32), AF.Identity, [f4, cn, kKc], scale=F(CN, 0, 1), bias=C(cKc, 0, 1))
         pl = act(T.places[:, t:t + 1], F(CN, 0, 1), AF.Copy, [cn], bias=float(M * r))
-        if t == R - 1:
+        if last:
             send(T.places[:, 0:R], [T.landp[:, R * r:R * r + R]] * 3, "xp", [pl])
         pkc = cp(p[:, :].bitcast(u32), m[:, 128:128 + M].bitcast(u32).indirect(oc[:, 0:8]), [lc] + mdeps)
         pks = act(ps[:, :], ms[:, 128:128 + M].indirect(oc[:, 0:8]), AF.Copy, [lc] + mdeps)
@@ -253,11 +258,14 @@ def rank_program(g, core, T, topo):
         for b in (0, 2):
             cast_prev.append(cp(h[:, b:512:4], T.pblend[:, 512 * b:512 * b + 128], [bl[b]]))
             cast_prev.append(act(h[:, b + 1:512:4], T.pblend[:, 512 * b + 512:512 * b + 640], AF.Copy, [bl[b + 1]]))
+        for b in (1, 2, 3):
+            kk = act(F(KF, 0, 128, 32 * b, 32 * b + 32), F(KF, 0, 128, 0, 32), AF.Copy, [kf])
         nd = qmx(m[:, 0:128], ms[:, 0:128], h[:, :], cast_prev)
         x1 = ("x1_%d" % t, 3 * ne)
-        MX, FL, MI, MR, AC, AN, KR = new(1), new(1), new(32), new(128), new(3), new(128), new(128)
+        MX, FL, MI, MR, AC, CS = new(1), new(1), new(32), new(128), new(3), new(128)
+        RW, S1, J3, BW, BT = RW3 + 8 * t, new(1), new(5), new(32), new(32)
         col = [land[:, s:s + 1] for s in range(4)]
-        me = F(RM, M - 1, M)
+        lo = act(land[:, r:r + 1], me, AF.Copy, [x1])
         if r == 0:
             x = red(F(MX, 0, 1), land[:, 1:4], OP.max, [x1])
             mi = ts(F(MI, 0, 32), F(OW, 0, 32), F(MX, 0, 1), OP.is_ge, deps=[x, ow])
@@ -272,18 +280,16 @@ def rank_program(g, core, T, topo):
             x = tt(F(MX, 0, 1), col[0], col[1], OP.max, [x1])
             x = ts(F(FL, 0, 1), me, col[3], OP.is_ge)
             mi = ts(F(MI, 0, 32), F(OW, 0, 32), F(MX, 0, 1), OP.is_gt, F(FL, 0, 1), OP.mult, deps=[x, ow])
-        lo = act(land[:, r:r + 1], me, AF.Copy, [x1])
         for a in range(4):
             x = tr(F(MR, 32 * a, 32 * a + 32, 0, 32), F(MI, 0, 32, 32 * a, 32 * a + 32), [mi])
-        CS = CSs[t]
-        cs = scan(F(CS, 8, 136, 0, 32), F(MR, 0, 128, 0, 32), C(cE, 0, 128, 0, 32), OP.add, OP.min, 0.0, [x, f2])
+        cs = scan(F(CS, 0, 128, 0, 32), F(MR, 0, 128, 0, 32), C(cE, 0, 128, 0, 32), OP.add, OP.min, 0.0, [x, f2])
         for c in range(3):
-            ac = act(F(new(128), 0, 128, 0, 32), F(CS, 8, 136, 0, 32), AF.Sign, [cs, kKb], scale=-1.0, bias=C(cKb, c, c + 1, 0, 32),
+            ac = act(F(new(128), 0, 128, 0, 32), F(CS, 0, 128, 0, 32), AF.Sign, [cs, kKb], scale=-1.0, bias=C(cKb, c, c + 1, 0, 32),
                      accum_out=F(AC, c, c + 1, 0, 32))
-        an = tt(F(AN, 0, 128, 0, 32), F(CS, 8, 136, 0, 32), F(CS, 7, 135, 0, 32), OP.subtract, [cs, fRW])
-        RW, S1, TC = RWs[t], new(1), new(1)
-        rw = scan(F(RW, 1, 5), land[:, 0:4], C(cNeg, 0, 4), OP.max, OP.max, -1e29, [lo, x1])
-        kr = tt(F(KR, 0, 128, 0, 32), F(AN, 0, 128, 0, 32), F(KF, 0, 128, 0, 32), OP.mult, [an, kf])
+        rw = scan(F(RW, 1, 5), land[:, 0:4], C(cNeg, 0, 4), OP.max, OP.max, -1e29, [lo, x1, fRW])
+        EQ, T1 = new(136), new(1)
+        s1 = act(F(J3, 0, 5), F(RW, 0, 5), AF.Sign, [rw], scale=-1.0, bias=F(RW, 4, 5), accum_out=F(S1, 0, 1))
+        bw = act(F(BW, 0, 32), C(cZero, 0, 32), AF.Identity, [s1], bias=F(S1, 0, 1))
         for a in range(4):
             lg = ts(og[32 * a:32 * a + 32, 0:3], F(AC, 0, 3, 0, 32), 0.5, OP.mult, 64.0, OP.add, deps=[ac])
         gc = cp(s_[:, :].bitcast(u32), m[:, :].bitcast(u32).indirect(og[:, 0:3]), [lg, nd])
@@ -292,79 +298,77 @@ def rank_program(g, core, T, topo):
         x2 = "x2_%d" % t
         send(s_[:, 0:E].bitcast(u8), [q[:, k0:k0 + E].bitcast(u8)] * 3, x2, [gc])
         send(ss_[:, 0:E], [qs[:, k0:k0 + E]] * 3, x2, [gs])
-        J3, BW, BT, EQ, P, Z, L = new(5), new(32), new(32), new(128), new(1), new(1), new(1)
-        s1 = act(F(J3, 0, 5), F(RW, 0, 5), AF.Sign, [rw], scale=-1.0, bias=F(RW, 4, 5), accum_out=F(S1, 0, 1))
-        bw = act(F(BW, 0, 32), C(cZero, 0, 32), AF.Identity, [s1], bias=F(S1, 0, 1))
-        tc = act(F(TC, 0, 1), F(S1, 0, 1), AF.Identity, [kJ48], scale=float(SL), bias=C(cJ48, 0, 1))
-        for b in (1, 2, 3):
-            kk = act(F(KR, 0, 128, 32 * b, 32 * b + 32), F(KR, 0, 128, 0, 32), AF.Copy, [kr])
-        AB = new(M)
-        ab = []
-        for c in range(3):
-            ab.append(act(F(AB, 128 * c, 128 * c + 128), F(KR, 0, 128), AF.Abs, [kk, kNp], bias=C(cNp, c, c + 1)))
+        need("y", gc, gs)
+        g.sync.dma_start(q[:, k0:k0 + SL].bitcast(u8), s_[:, :].bitcast(u8)).then_inc(sem["own%d" % t], 16)
+        g.sync.dma_start(qs[:, k0:k0 + SL], ss_[:, :]).then_inc(sem["own%d" % t], 16)
+        KG, AB, P, L, B2, R3, R4, LQ = new(SL), new(3 * SL), new(1), new(1), new(32), new(128), new(128), new(8)
+        D, BM, R5, R6, LM = new(3), new(96), new(96), new(96), new(24)
+        kg = act(F(KG, 0, SL), F(KF, 0, 136).indirect(og[:, 0:3]), AF.Copy, [kk, fKF])
+        ab = [act(F(AB, SL * c, SL * c + SL), F(KG, 0, SL), AF.Abs, [kg, kNp], bias=C(cNp, c, c + 1)) for c in range(3)]
+        tc = act(F(EQ, 128, 129), F(S1, 0, 1), AF.Identity, [kT, s1], scale=float(SL), bias=C(cT0, 0, 1))
+        tc = act(F(T1, 0, 1), F(S1, 0, 1), AF.Identity, scale=float(SL), bias=C(cT1, 0, 1))
         bt = ts(F(BT, 0, 32), C(cTri, 0, 32), F(S1, 0, 1), OP.min, deps=[s1, kTri])
         for b in range(1, 4):
             for a in range(b):
                 x = tr(F(WR, 32 + 32 * a, 64 + 32 * a, 32 * b, 32 * b + 32), F(BW, 0, 32, 32 * a, 32 * a + 32), [bw, fWR])
         x = tr(F(WR, 0, 32), F(BT, 0, 32), [bt])
-        x = ts(F(EQ, 0, 128), F(WR, 0, 128), F(S1, 0, 1), OP.is_equal, deps=[x])
-        x = red(F(P, 0, 1), F(EQ, 0, 128), OP.add, [x])
-        z = ts(F(A3, t, t + 1), F(P, 0, 1), float(E), OP.is_le, deps=[x])
-        z = tt(F(Z, 0, 1), F(P, 0, 1), F(TC, 0, 1), OP.add, [tc])
-        z = ts(F(L, 0, 1), F(Z, 0, 1), F(A3, t, t + 1), OP.mult, C(cJ, 0, 1), OP.add, deps=[z])
-        B2, R3, R4 = new(32), new(128), new(128)
+        d = [red(F(D, c, c + 1), F(AB, SL * c, SL * c + SL), OP.min, [ab[c]]) for c in range(3)]
+        eq = ts(F(EQ, 0, 128), F(WR, 0, 128), F(S1, 0, 1), OP.is_equal, deps=[x])
+        pz = act(F(new(136), 0, 129), F(EQ, 0, 129), AF.Copy, [eq, tc], accum_out=F(P, 0, 1))
+        for c in range(3):
+            bm = ts(F(BM, 32 * c, 32 * c + 32), C(cMask, 0, 32), F(D, c, c + 1), OP.min, C(cPl, c, c + 1), OP.min, deps=[d[c]])
+        oh = ts(F(OH, t, 12, st=3), C(cFour, 0, 4), F(S1, 0, 1), OP.is_equal, deps=[i3])
+        y = tr(F(R5, 0, 96), F(BM, 0, 96), [bm])
+        z = ts(F(A3, t, t + 1), F(P, 0, 1), F(T1, 0, 1), OP.is_le, deps=[pz, tc])
+        y = scan(F(R6, 0, 96), C(cKeep, 0, 96), F(R5, 0, 96), OP.mult, OP.add, 0.0, [y])
+        z = ts(F(L, 0, 1), F(P, 0, 1), F(A3, t, t + 1), OP.mult, C(cJ, 0, 1), OP.add, deps=[z])
+        for b in (1, 2, 3):
+            for a in range(4):
+                lms = act(F(LM, 6 * a, 6 * a + 6, 32 * b, 32 * b + 32), F(R6, 15, 96, 32 * a, 32 * a + 32, 16), AF.Copy, [y])
+        for a in range(2):
+            lmv = cp(F(LM, 6 * a, 6 * a + 6, 0, 32), F(R6, 15, 96, 32 * a, 32 * a + 32, 16), [y])
         z = ts(F(B2, 0, 32), C(cMask, 0, 32), F(L, 0, 1), OP.min, deps=[z])
+        for a in range(2, 4):
+            lmv = cp(F(LM, 6 * a, 6 * a + 6, 0, 32), F(R6, 15, 96, 32 * a, 32 * a + 32, 16), [y])
         for a in range(4):
             x = tr(F(R3, 32 * a, 32 * a + 32, 0, 32), F(B2, 0, 32, 32 * a, 32 * a + 32), [z])
         x = scan(F(R4, 0, 128, 0, 32), C(cKeep, 0, 128, 0, 32), F(R3, 0, 128, 0, 32), OP.mult, OP.add, 0.0, [x])
-        for a in range(4):
-            lq = cp(oq[32 * a:32 * a + 32, 0:8], F(R4, 15, 128, 0, 32, 16), [x])
-        D, BM, R5, R6 = new(3), new(96), new(M), new(M)
-        for c in range(3):
-            d = red(F(D, c, c + 1), F(AB, 128 * c, 128 * c + 128), OP.min, [ab[c]])
-        for c in range(3):
-            x = ts(F(BM, 32 * c, 32 * c + 32), C(cMask, 0, 32), F(D, c, c + 1), OP.min, C(cPl, c, c + 1), OP.min, deps=[("cv", d[1] - 2 + c)])
-        for a in range(4):
-            y = tr(F(R5, 96 * a, 96 * a + 96, 0, 32), F(BM, 0, 96, 32 * a, 32 * a + 32), [x])
-        x = scan(F(R6, 0, M, 0, 32), C(cKeep, 0, M, 0, 32), F(R5, 0, M, 0, 32), OP.mult, OP.add, 0.0, [y])
-        for a in range(4):
-            lm = cp(om[32 * a:32 * a + 32, 0:24], F(R6, 15, M, 0, 32, 16), [x])
-        oh = ts(F(OH, t, 12, st=3), C(cFour, 0, 4), F(S1, 0, 1), OP.is_equal, deps=[i3])
-        gc = cp(q[:, k0:k0 + SL].bitcast(u32), m[:, :].bitcast(u32).indirect(og[:, 0:3]))
-        gs = act(qs[:, k0:k0 + SL], ms[:, :].indirect(og[:, 0:3]), AF.Copy)
-        if t < R - 1:
+        for b in range(4):
+            lqs = act(F(LQ, 0, 8, 32 * b, 32 * b + 32), F(R4, 15, 128, 0, 32, 16), AF.Copy, [x])
+        lm = cp(om[:, :], F(LM, 0, 24), [lms, lmv])
+        if not last:
             m2, ms2, c0 = T["m%d" % (t + 1)], T["ms%d" % (t + 1)], 128
         else:
             m2, ms2, c0 = T.m3, T.ms3, 0
         mc = cp(m2[:, c0:c0 + M].bitcast(u32), m[:, :].bitcast(u32).indirect(om[:, 0:24]), [lm, nd] + mdeps)
         mp = act(ms2[:, c0:c0 + M], ms[:, :].indirect(om[:, 0:24]), AF.Copy, [lm, nd] + mdeps)
         mdeps = [mc, mp]
-        if t == R - 1:
+        lq = cp(oq[:, :], F(LQ, 0, 8), [lqs])
+        if last:
             need("y", mc, mp)
             g.sync.dma_start(T.oc[:, :], T.m3[:, :].bitcast(u8)).then_inc(sem.out, 16)
             for k in range(4):
                 g.sync.dma_start(T.osc[4 * k:4 * k + 4, :], T.ms3[32 * k:32 * k + 4, :]).then_inc(sem.out, 16)
-            xp = ("xp", 3 * ne)
-            lp = act(T.landp[:, R * r:R * r + R], T.places[:, 0:R], AF.Copy, [xp, pl])
-            G12, G3, SG, AM, W1, WO = new(12), new(3), new(3), new(3), new(3), new(3)
-            sg = ts(F(SG, 0, 3), F(A3, 0, 3), 2.0, OP.mult, -1.0, OP.add)
-            sg = ts(F(AM, 0, 3), F(A3, 0, 3), -1.0, OP.add)
-            x = tt(F(G12, 0, 12), F(OH, 0, 12), T.landp[:, :], OP.mult, [oh, lp, xp])
-            for c in range(3):
-                x2_ = red(F(G3, c, c + 1), F(G12, c, 12, st=3), OP.add, [x])
-            x = tt(F(W1, 0, 3), F(G3, 0, 3), F(SG, 0, 3), OP.mult, [x2_])
-            x = tt(F(WO, 0, 3), F(W1, 0, 3), F(AM, 0, 3), OP.add, [x])
-            need("y", x)
-            for c in range(R):
-                g.sync.dma_start(T.wi[c:c + 1, :], F(WO, c, c + 1)).then_inc(sem.out, 16)
+            SG, AM = new(3), new(3)
+            lp = act(T.landp[:, R * r:R * r + R], T.places[:, 0:R], AF.Copy, [("xp", 3 * ne), pl])
+            sg = act(F(SG, 0, 3), F(A3, 0, 3), AF.Copy, [z], scale=2.0, bias=-1.0)
+            sg = act(F(AM, 0, 3), F(A3, 0, 3), AF.Copy, scale=1.0, bias=-1.0)
         q2, qs2 = T["q%d" % (t + 1)], T["qs%d" % (t + 1)]
-        xx = (x2, 2 * 3 * ne)
-        a = cp(q2[:, 0:128].bitcast(u32), q[:, :].bitcast(u32).indirect(oq[:, 0:8]), [lq, gc, xx] + qdeps)
-        b = act(qs2[:, 0:128], qs[:, :].indirect(oq[:, 0:8]), AF.Copy, [lq, gs, xx] + qdeps)
-        qdeps = [a, b]
+        ready = [lq, (x2, 2 * 3 * ne), ("own%d" % t, 32)] + qdeps
+        qdeps = [cp(q2[:, 0:128].bitcast(u32), q[:, :].bitcast(u32).indirect(oq[:, 0:8]), ready),
+                 act(qs2[:, 0:128], qs[:, :].indirect(oq[:, 0:8]), AF.Copy, ready)]
     y = mm(T.py[:, 0:128], T.wq[:, :], T.ws[:, :], T.q3[:, :], T.qs3[:, :], True, True, [kw] + qdeps)
+    G12, G3, W1, WO = new(12), new(3), new(3), new(3)
+    x = tt(F(G12, 0, 12), F(OH, 0, 12), T.landp[:, :], OP.mult, [oh, lp, ("xp", 3 * ne)])
+    for c in range(3):
+        w = red(F(G3, c, c + 1), F(G12, c, 12, st=3), OP.add, [x])
     y = cp(T.yo[:, :], T.py[:, 0:128], [y])
+    x = tt(F(W1, 0, 3), F(G3, 0, 3), F(SG, 0, 3), OP.mult, [w, sg])
+    x = tt(F(WO, 0, 3), F(W1, 0, 3), F(AM, 0, 3), OP.add, [x])
     need("y", y)
     g.sync.dma_start(T.y[:, :], T.yo[:, :]).then_inc(sem.out, 16)
+    need("s", x)
+    for c in range(R):
+        S.dma_start(T.wi[c:c + 1, :], F(WO, c, c + 1)).then_inc(sem.out, 16)
     need("y", ("out", 16 * (1 + 4 + R + 1)))
     need("g", ("loc", local[0]), *[("c" + k, n) for k, n in count.items()])

@@ -4,7 +4,7 @@ from concourse.mybir import dt, AluOpType, ActivationFunctionType, AxisListType
 M, A, E, R = 384, 32, 40, 3
 HM = M // 2
 SL = 48
-QW = 128 + 4 * SL
+QW, QL = 128 + 4 * SL, 128 + 4 * 128
 FW = 14000
 CODE, U8, F32, BF, I32, U16 = "float8_e4m3fn_x4", "uint8", "float32", "bfloat16", "int32", "uint16"
 
@@ -14,7 +14,7 @@ SCRATCH = {
     "wt": ("sbuf", [128, 512], BF), "wq": ("sbuf", [128, 128], CODE), "ws": ("sbuf", [128, 128], U8),
     "ce": ("sbuf", [128, 520 + 1024], F32), "et": ("sbuf", [128, 2048], BF), "eq": ("sbuf", [128, 512], CODE), "es": ("sbuf", [128, 512], U8),
     "ints": ("sbuf", [128, 64], I32),
-    "cf": ("sbuf", [128, 1000], F32),
+    "cf": ("sbuf", [128, 1100], F32),
     "ff": ("sbuf", [128, FW], F32),
     "offx": ("sbuf", [128, 2], U16),
     "places": ("sbuf", [128, 4], F32), "landp": ("sbuf", [128, 12], F32),
@@ -25,13 +25,14 @@ SCRATCH = {
 }
 SEMAPHORES = ["cv", "cs", "ct", "cg", "lx", "lm", "lw", "x0", "xp", "loc", "out"]
 for _t in range(R):
+    _w = QL if _t == R - 1 else QW
     SCRATCH.update({
         "m%d" % _t: ("sbuf", [128, 128 + M], CODE), "ms%d" % _t: ("sbuf", [128, 128 + M], U8),
-        "q%d" % _t: ("sbuf", [128, QW], CODE), "qs%d" % _t: ("sbuf", [128, QW], U8),
+        "q%d" % _t: ("sbuf", [128, _w], CODE), "qs%d" % _t: ("sbuf", [128, _w], U8),
         "p%d" % _t: ("sbuf", [128, 128], CODE), "ps%d" % _t: ("sbuf", [128, 128], U8),
         "s%d" % _t: ("sbuf", [128, SL], CODE), "ss%d" % _t: ("sbuf", [128, SL], U8),
         "h%d" % _t: ("sbuf", [128, 512], BF),
-        "land%d" % _t: ("sbuf", [128, 4], F32),
+        "land%d" % _t: ("sbuf", [128, 8], F32),
         "oc%d" % _t: ("sbuf", [128, 8], U16), "og%d" % _t: ("sbuf", [128, 4], U16),
         "oq%d" % _t: ("sbuf", [128, 8], U16), "om%d" % _t: ("sbuf", [128, 24], U16),
     })
@@ -152,61 +153,62 @@ def rank_program(g, core, T, topo):
 
     small = {"allow_small_or_imprecise_dtypes": True}
     cRow, cFour = cnew(32), cnew(4)
-    i0 = io(T.ints[:, 0:1], [[0, 1]], 0, 1)
-    i1 = io(T.ints[:, 16:48], [[1, 32]], 128, -1)
-    i2 = io(C(cRow, 0, 32), [[1, 32]], 0, 0, **small)
-    i3 = io(C(cFour, 0, 4), [[1, 4]], 1, 0, **small)
-    i4 = io(T.ce[:, 512:516], [[1, 4]], 0, 4, **small)
-    i5 = io(T.ce[:, 0:512], [[1, 512]], 0, 0, **small)
-    z0 = fill(T.xt[:, 4 * A:512], 0.0)
     cNeg, cKeep, cE, cZero, c2k = cnew(HM), cnew(128), cnew(128), cnew(32), cnew(32)
     cJ, cM16, cKb, cKc, cT0, cT1, cPl, cNp, cP31, cB = [cnew(n) for n in (1, 1, 3, 1, 1, 1, 3, 3, 1, 1)]
-    cMask, cTri = cnew(32), cnew(32)
-    a0 = cp(C(cJ, 0, 1), T.ints[:, 0:1], [i0])
-    b0 = ts(T.ints[:, 1:2], T.ints[:, 0:1], 15, OP.bitwise_and)
+    cMask, cTri, cNm = cnew(32), cnew(32), cnew(32)
+    i0 = io(T.ints[:, 0:1], [[0, 1]], 0, 1)
+    i5 = io(T.ce[:, 0:512], [[1, 512]], 0, 0, **small)
+    i4 = io(T.ce[:, 512:516], [[1, 4]], 0, 4, **small)
+    z0 = fill(T.xt[:, 4 * A:512], 0.0)
+    b0 = ts(T.ints[:, 1:2], T.ints[:, 0:1], 15, OP.bitwise_and, deps=[i0])
+    a0 = cp(C(cJ, 0, 1), T.ints[:, 0:1])
     b1 = ts(T.ints[:, 2:3], T.ints[:, 0:1], 31, OP.bitwise_and)
     b2 = ts(T.ints[:, 3:4], T.ints[:, 0:1], 5, OP.arith_shift_right)
-    b3 = ts(T.ints[:, 16:48], T.ints[:, 16:48], 15, OP.bitwise_and, deps=[i1])
     a1 = cp(C(cM16, 0, 1), T.ints[:, 1:2], [b0])
-    a2 = cp(C(cP31, 0, 1), T.ints[:, 2:3], [b1])
-    a3_ = ts(C(cB, 0, 1), T.ints[:, 3:4], 64.0, OP.mult, deps=[b2])
     for c in range(3):
         kKb = ts(C(cKb, c, c + 1), C(cM16, 0, 1), 16.0 * c + 0.5, OP.add, deps=[a1])
     kOx = ts(T.offx[:, 0:2], C(cKb, 0, 2), -0.5, OP.add, deps=[kKb])
-
     qx = qmx(T.xq[:, :], T.xs[:, :], T.xt[:, :], [("lx", 16), z0])
     o0, o1 = A * r, A * r + A
     send(T.xq[:, 0:A].bitcast(u8), [T.q0[:, o0:o1].bitcast(u8)] * 3, "x0", [qx])
     send(T.xs[:, 0:A], [T.qs0[:, o0:o1]] * 3, "x0", [qx])
+    i1 = io(T.ints[:, 16:48], [[1, 32]], 128, -1)
+    i2 = io(C(cRow, 0, 32), [[1, 32]], 0, 0, **small)
+    i3 = io(C(cFour, 0, 4), [[1, 4]], 1, 0, **small)
     own = cp(T.q0[:, o0:o1].bitcast(u32), T.xq[:, :].bitcast(u32).indirect(T.offx[:, 0:2]), [kOx, qx])
     owns = act(T.qs0[:, o0:o1], T.xs[:, :].indirect(T.offx[:, 0:2]), AF.Copy, [kOx, qx])
     ke = []
     for b in range(2):
         x = act(T.ce[:, 520 + 512 * b:1032 + 512 * b], T.ce[:, 0:512], AF.Abs, [i4, i5], scale=-1.0, bias=T.ce[:, 512 + b:513 + b])
         ke.append(act(T.et[:, 512 * b:512 * b + 512], T.ce[:, 520 + 512 * b:1032 + 512 * b], AF.Relu, [x], scale=-1.0, bias=0.5))
+    a2 = cp(C(cP31, 0, 1), T.ints[:, 2:3], [b1])
+    a3_ = ts(C(cB, 0, 1), T.ints[:, 3:4], 64.0, OP.mult, deps=[b2])
     f0 = fill(C(cNeg, 0, HM), -1e29)
     f1 = fill(C(cKeep, 0, 128), 1.0)
     f2 = fill(C(cE, 0, 128), float(E))
     f3 = fill(C(cZero, 0, 32), 0.0)
     memd = qmx(T.m0[:, 128:128 + M], T.ms0[:, 128:128 + M], T.met[:, :], [("lm", 32)])
+    for b in (2, 3):
+        ke.append(ts(T.et[:, 512 * b:512 * b + 512], T.ce[:, 0:512], T.ce[:, 512 + b:513 + b], OP.is_equal, 0.5, OP.mult, deps=[i4, i5]))
     f4 = fill(C(c2k, 0, 32), 2048.0)
     need("v", f1)
     f1 = fill(C(cKeep, 0, 128, st=16), 0.0)
-    for b in (2, 3):
-        ke.append(ts(T.et[:, 512 * b:512 * b + 512], T.ce[:, 0:512], T.ce[:, 512 + b:513 + b], OP.is_equal, 0.5, OP.mult, deps=[i4, i5]))
-    kmask = ts(C(cMask, 0, 32), T.ints[:, 16:48], 0.0, OP.is_equal, 1e6, OP.mult, deps=[b3])
+    b3 = ts(T.ints[:, 16:48], T.ints[:, 16:48], 15, OP.bitwise_and, deps=[i1])
     kKc = ts(C(cKc, 0, 1), C(cJ, 0, 1), 2048.0, OP.add, deps=[a0])
     kT = ts(C(cT0, 0, 1), C(cJ, 0, 1), -1.0, OP.mult, float(127 - SL), OP.add)
     kT = ts(C(cT1, 0, 1), C(cJ, 0, 1), -1.0, OP.mult, float(127 - SL + E), OP.add)
+    kmask = ts(C(cMask, 0, 32), T.ints[:, 16:48], 0.0, OP.is_equal, 1e6, OP.mult, deps=[b3])
     for h in range(3):
         kPl = ts(C(cPl, h, h + 1), C(cB, 0, 1), C(cJ, 0, 1), OP.add, 128.0 + 32 * h, OP.add, deps=[a3_])
     kTri = ts(C(cTri, 0, 32), C(cRow, 0, 32), C(cP31, 0, 1), OP.is_ge, 1e6, OP.mult, deps=[a2, i2])
+    kNm = ts(C(cNm, 0, 32), C(cMask, 0, 32), float(HM) - 1e6, OP.add, deps=[kmask])
     kNp = ts(C(cNp, 0, 3), C(cPl, 0, 3), -127.0, OP.add, -2048.0, OP.mult, deps=[kPl])
     ke = qmx(T.eq[:, :], T.es[:, :], T.et[:, :], ke)
-    WR, OH, A3, KF, RW3 = new(128), new(12), new(3), new(136), new(8 * R)
+    WR, OH, A3, KF, K2, RW3 = new(128), new(12), new(3), new(136), new(136), new(16 * R)
     fWR = fill(F(WR, 0, 128), 0.0)
     fKF = fill(F(KF, 128, 136), 0.0)
-    fRW = fill(F(RW3, 0, 8 * R), -1e29)
+    fK2 = fill(F(K2, 128, 136), -128.0)
+    fRW = fill(F(RW3, 0, 16 * R), -1e29)
     kw = qmx(T.wq[:, :], T.ws[:, :], T.wt[:, :], [("lw", 16)])
 
     qdeps = [own, owns, ("x0", 2 * ne * 3)]
@@ -219,29 +221,38 @@ def rank_program(g, core, T, topo):
         h = T["h%d" % t]
         oc, og, oq, om = T["oc%d" % t], T["og%d" % t], T["oq%d" % t], T["om%d" % t]
         last = t == R - 1
-        RM, JK, CN = new(M), new(M), new(1)
-        me = F(RM, M - 1, M)
-        sc = []
+        x1, x2 = "x1_%d" % t, "x2_%d" % t
+        RM, JK, CN, C0, C1 = new(M), new(M), new(1), new(1), new(1)
+        half = [F(RM, k, M, st=2) for k in range(2)]
+        top = [F(RM, M - 2 + k, M - 1 + k) for k in range(2)]
+        rm = []
         for k in range(2):
-            sc.append(mm(T.pscore[:, 512 * k:512 * k + HM], q[:, 0:128], qs[:, 0:128], m[:, 128 + HM * k:128 + HM * k + HM],
+            rm.append(mm(T.pscore[:, 512 * k:512 * k + HM], q[:, 0:128], qs[:, 0:128], m[:, 128 + HM * k:128 + HM * k + HM],
                          ms[:, 128 + HM * k:128 + HM * k + HM], True, True, qdeps + mdeps + [scan_prev[k]]))
-        rm = scan(F(RM, 0, HM), T.pscore[:, 0:HM], C(cNeg, 0, HM), OP.max, OP.max, -1e29, [sc[0], f0])
-        rm2 = scan(F(RM, HM, M), T.pscore[:, 512:512 + HM], C(cNeg, 0, HM), OP.max, OP.max, F(RM, HM - 1, HM), [sc[1], rm])
-        scan_prev, rm = [rm, rm2], rm2
-        send(me, [land[:, r:r + 1]] * 3, "x1_%d" % t, [rm])
+        rm = [scan(half[k], T.pscore[:, 512 * k:512 * k + HM], C(cNeg, 0, HM), OP.max, OP.max, -1e29, [rm[k], f0]) for k in range(2)]
+        scan_prev = rm
+        send(F(RM, M - 2, M), [land[:, 2 * r:2 * r + 2]] * 3, x1, rm)
         for b in range(4):
             dq = mm(T.pblend[:, 512 * b:512 * b + 128], T.eq[:, 128 * b:128 * b + 128], T.es[:, 128 * b:128 * b + 128],
                     q[:, 0:128], qs[:, 0:128], True, False, [ke] + cast_prev)
-        cn = act(F(JK, 0, M), F(RM, 0, M), AF.Sign, [rm], scale=-1.0, bias=me, accum_out=F(CN, 0, 1))
-        B1, R1, R2 = new(32), new(128), new(128)
-        bc = ts(F(B1, 0, 32), C(cMask, 0, 32), F(CN, 0, 1), OP.min, deps=[cn, kmask])
+        B1, R1, R2, FC, K1, BA, NM, ME = new(32), new(128), new(128), new(1), new(1), new(1), new(32), new(1)
+        c0_ = act(F(JK, 0, HM), half[0], AF.Sign, [rm[0]], scale=-1.0, bias=top[0], accum_out=F(C0, 0, 1))
+        c1_ = act(F(JK, HM, M), half[1], AF.Sign, [rm[1]], scale=-1.0, bias=top[1], accum_out=F(C1, 0, 1))
+        k1 = ts(F(K1, 0, 1), top[1], top[0], OP.is_le, 1e5, OP.mult, deps=rm)
+        fc = ts(F(FC, 0, 1), top[1], top[0], OP.is_gt, 1e5, OP.mult)
+        mx = tt(F(ME, 0, 1), top[0], top[1], OP.max)
+        nm = ts(F(NM, 0, 32), C(cNm, 0, 32), F(K1, 0, 1), OP.add, deps=[k1, kNm])
+        ba = ts(F(BA, 0, 1), F(FC, 0, 1), F(C0, 0, 1), OP.add, deps=[fc, c0_])
+        bc = ts(F(B1, 0, 32), F(NM, 0, 32), F(C1, 0, 1), OP.add, F(BA, 0, 1), OP.min, deps=[nm, ba, c1_])
         for a in range(4):
             x = tr(F(R1, 32 * a, 32 * a + 32, 0, 32), F(B1, 0, 32, 32 * a, 32 * a + 32), [bc])
-        x = scan(F(R2, 0, 128, 0, 32), C(cKeep, 0, 128, 0, 32), F(R1, 0, 128, 0, 32), OP.mult, OP.add, 0.0, [x, f1])
+        k1 = ts(F(K1, 0, 1), F(K1, 0, 1), float(HM), OP.add)
+        x = scan(F(R2, 0, 128, 0, 32), C(cKeep, 0, 128, 0, 32), F(R1, 0, 128, 0, 32), OP.mult, OP.max, 0.0, [x, f1])
+        cn = ts(F(CN, 0, 1), F(C1, 0, 1), F(K1, 0, 1), OP.add, F(BA, 0, 1), OP.min, deps=[k1])
         for a in range(4):
             lc = cp(oc[32 * a:32 * a + 32, 0:8], F(R2, 15, 128, 0, 32, 16), [x])
         OW, KB = new(32), new(32)
-        ow = act(F(OW, 0, 32), C(cZero, 0, 32), AF.Identity, [f3], bias=me)
+        ow = act(F(OW, 0, 32), C(cZero, 0, 32), AF.Identity, [f3, mx], bias=F(ME, 0, 1))
         kb = act(F(KB, 0, 32), C(c2k, 0, 32), AF.Identity, [f4, cn, kKc], scale=F(CN, 0, 1), bias=C(cKc, 0, 1))
         pl = act(T.places[:, t:t + 1], F(CN, 0, 1), AF.Copy, [cn], bias=float(M * r))
         if last:
@@ -256,57 +267,67 @@ def rank_program(g, core, T, topo):
                          p[:, :], ps[:, :], False, True, [pkc, pks]))
         cast_prev = []
         for b in (0, 2):
-            cast_prev.append(cp(h[:, b:512:4], T.pblend[:, 512 * b:512 * b + 128], [bl[b]]))
-            cast_prev.append(act(h[:, b + 1:512:4], T.pblend[:, 512 * b + 512:512 * b + 640], AF.Copy, [bl[b + 1]]))
+            cast_prev.append(act(h[:, b:512:4], T.pblend[:, 512 * b:512 * b + 128], AF.Copy, [bl[b]]))
+            cast_prev.append(cp(h[:, b + 1:512:4], T.pblend[:, 512 * b + 512:512 * b + 640], [bl[b + 1]]))
         for b in (1, 2, 3):
             kk = act(F(KF, 0, 128, 32 * b, 32 * b + 32), F(KF, 0, 128, 0, 32), AF.Copy, [kf])
         nd = qmx(m[:, 0:128], ms[:, 0:128], h[:, :], cast_prev)
-        x1 = ("x1_%d" % t, 3 * ne)
+        if last:
+            k0 = 128 + 128 * r
+            send(m[:, 0:128].bitcast(u8), [q[:, k0:k0 + 128].bitcast(u8)] * 3, x2, [nd])
+            send(ms[:, 0:128], [qs[:, k0:k0 + 128]] * 3, x2, [nd])
+            need("y", nd)
+            g.sync.dma_start(q[:, k0:k0 + 128].bitcast(u8), m[:, 0:128].bitcast(u8)).then_inc(sem["own%d" % t], 16)
+            g.sync.dma_start(qs[:, k0:k0 + 128], ms[:, 0:128]).then_inc(sem["own%d" % t], 16)
+        x1 = (x1, 3 * ne)
         MX, FL, MI, MR, AC, CS = new(1), new(1), new(32), new(128), new(3), new(128)
-        RW, S1, J3, BW, BT = RW3 + 8 * t, new(1), new(5), new(32), new(32)
-        col = [land[:, s:s + 1] for s in range(4)]
-        lo = act(land[:, r:r + 1], me, AF.Copy, [x1])
+        RW, S1, J3, BW, BT = RW3 + 16 * t, new(1), new(5), new(32), new(32)
+        lo = act(land[:, 2 * r:2 * r + 2], F(RM, M - 2, M), AF.Copy, [x1])
         if r == 0:
-            x = red(F(MX, 0, 1), land[:, 1:4], OP.max, [x1])
+            x = red(F(MX, 0, 1), land[:, 2:8], OP.max, [x1])
             mi = ts(F(MI, 0, 32), F(OW, 0, 32), F(MX, 0, 1), OP.is_ge, deps=[x, ow])
         elif r == 3:
-            x = red(F(MX, 0, 1), land[:, 0:3], OP.max, [x1])
+            x = red(F(MX, 0, 1), land[:, 0:6], OP.max, [x1])
             mi = ts(F(MI, 0, 32), F(OW, 0, 32), F(MX, 0, 1), OP.is_gt, deps=[x, ow])
         elif r == 1:
-            x = tt(F(MX, 0, 1), col[2], col[3], OP.max, [x1])
-            x = ts(F(FL, 0, 1), me, col[0], OP.is_gt)
+            x = red(F(MX, 0, 1), land[:, 4:8], OP.max, [x1])
+            x = ts(F(FL, 0, 1), land[:, 0:1], land[:, 1:2], OP.max, F(ME, 0, 1), OP.is_lt, deps=[mx])
             mi = ts(F(MI, 0, 32), F(OW, 0, 32), F(MX, 0, 1), OP.is_ge, F(FL, 0, 1), OP.mult, deps=[x, ow])
         else:
-            x = tt(F(MX, 0, 1), col[0], col[1], OP.max, [x1])
-            x = ts(F(FL, 0, 1), me, col[3], OP.is_ge)
+            x = red(F(MX, 0, 1), land[:, 0:4], OP.max, [x1])
+            x = ts(F(FL, 0, 1), land[:, 6:7], land[:, 7:8], OP.max, F(ME, 0, 1), OP.is_le, deps=[mx])
             mi = ts(F(MI, 0, 32), F(OW, 0, 32), F(MX, 0, 1), OP.is_gt, F(FL, 0, 1), OP.mult, deps=[x, ow])
         for a in range(4):
             x = tr(F(MR, 32 * a, 32 * a + 32, 0, 32), F(MI, 0, 32, 32 * a, 32 * a + 32), [mi])
         cs = scan(F(CS, 0, 128, 0, 32), F(MR, 0, 128, 0, 32), C(cE, 0, 128, 0, 32), OP.add, OP.min, 0.0, [x, f2])
-        for c in range(3):
+        for c in range(2):
             ac = act(F(new(128), 0, 128, 0, 32), F(CS, 0, 128, 0, 32), AF.Sign, [cs, kKb], scale=-1.0, bias=C(cKb, c, c + 1, 0, 32),
                      accum_out=F(AC, c, c + 1, 0, 32))
-        rw = scan(F(RW, 1, 5), land[:, 0:4], C(cNeg, 0, 4), OP.max, OP.max, -1e29, [lo, x1, fRW])
+        x = ts(F(K2, 0, 128, 0, 32), F(CS, 0, 128, 0, 32), C(cKb, 2, 3, 0, 32), OP.is_le, 2.0, OP.mult, deps=[cs, kKb])
+        rw = scan(F(RW, 1, 9), land[:, 0:8], C(cNeg, 0, 8), OP.max, OP.max, -1e29, [lo, x1, fRW])
+        av = red(F(AC, 2, 3, 0, 32), F(K2, 0, 129, 0, 32), OP.add, [x, fK2])
         EQ, T1 = new(136), new(1)
-        s1 = act(F(J3, 0, 5), F(RW, 0, 5), AF.Sign, [rw], scale=-1.0, bias=F(RW, 4, 5), accum_out=F(S1, 0, 1))
+        s1 = act(F(J3, 0, 5), F(RW, 0, 9, st=2), AF.Sign, [rw], scale=-1.0, bias=F(RW, 8, 9), accum_out=F(S1, 0, 1))
         bw = act(F(BW, 0, 32), C(cZero, 0, 32), AF.Identity, [s1], bias=F(S1, 0, 1))
         for a in range(4):
-            lg = ts(og[32 * a:32 * a + 32, 0:3], F(AC, 0, 3, 0, 32), 0.5, OP.mult, 64.0, OP.add, deps=[ac])
-        gc = cp(s_[:, :].bitcast(u32), m[:, :].bitcast(u32).indirect(og[:, 0:3]), [lg, nd])
-        gs = act(ss_[:, :], ms[:, :].indirect(og[:, 0:3]), AF.Copy, [lg, nd])
-        k0 = 128 + SL * r
-        x2 = "x2_%d" % t
-        send(s_[:, 0:E].bitcast(u8), [q[:, k0:k0 + E].bitcast(u8)] * 3, x2, [gc])
-        send(ss_[:, 0:E], [qs[:, k0:k0 + E]] * 3, x2, [gs])
-        need("y", gc, gs)
-        g.sync.dma_start(q[:, k0:k0 + SL].bitcast(u8), s_[:, :].bitcast(u8)).then_inc(sem["own%d" % t], 16)
-        g.sync.dma_start(qs[:, k0:k0 + SL], ss_[:, :]).then_inc(sem["own%d" % t], 16)
-        KG, AB, P, L, B2, R3, R4, LQ = new(SL), new(3 * SL), new(1), new(1), new(32), new(128), new(128), new(8)
-        D, BM, R5, R6, LM = new(3), new(96), new(96), new(96), new(24)
-        kg = act(F(KG, 0, SL), F(KF, 0, 136).indirect(og[:, 0:3]), AF.Copy, [kk, fKF])
+            lg = ts(og[32 * a:32 * a + 32, 0:3], F(AC, 0, 3, 0, 32), 0.5, OP.mult, 64.0, OP.add, deps=[ac, av])
+        if not last:
+            gc = cp(s_[:, :].bitcast(u32), m[:, :].bitcast(u32).indirect(og[:, 0:3]), [lg, nd])
+            gs = act(ss_[:, :], ms[:, :].indirect(og[:, 0:3]), AF.Copy, [lg, nd])
+            k0 = 128 + SL * r
+            send(s_[:, 0:E].bitcast(u8), [q[:, k0:k0 + E].bitcast(u8)] * 3, x2, [gc])
+            send(ss_[:, 0:E], [qs[:, k0:k0 + E]] * 3, x2, [gs])
+            need("y", gc, gs)
+            g.sync.dma_start(q[:, k0:k0 + SL].bitcast(u8), s_[:, :].bitcast(u8)).then_inc(sem["own%d" % t], 16)
+            g.sync.dma_start(qs[:, k0:k0 + SL], ss_[:, :]).then_inc(sem["own%d" % t], 16)
+        KG, AB, P, L, B2, R3, R4 = new(SL), new(3 * SL), new(1), new(1), new(32), new(128), new(128)
+        D, BM, R5, R6, LM, PS = new(3), new(96), new(96), new(96), new(24), new(1)
+        kg = act(F(KG, 0, SL), F(KF, 0, 136).indirect(og[:, 0:3]), AF.Copy, [kk, fKF, lg])
         ab = [act(F(AB, SL * c, SL * c + SL), F(KG, 0, SL), AF.Abs, [kg, kNp], bias=C(cNp, c, c + 1)) for c in range(3)]
         tc = act(F(EQ, 128, 129), F(S1, 0, 1), AF.Identity, [kT, s1], scale=float(SL), bias=C(cT0, 0, 1))
         tc = act(F(T1, 0, 1), F(S1, 0, 1), AF.Identity, scale=float(SL), bias=C(cT1, 0, 1))
+        if last:
+            tc = act(F(PS, 0, 1), F(S1, 0, 1), AF.Copy, scale=128.0)
         bt = ts(F(BT, 0, 32), C(cTri, 0, 32), F(S1, 0, 1), OP.min, deps=[s1, kTri])
         for b in range(1, 4):
             for a in range(b):
@@ -321,54 +342,51 @@ def rank_program(g, core, T, topo):
         y = tr(F(R5, 0, 96), F(BM, 0, 96), [bm])
         z = ts(F(A3, t, t + 1), F(P, 0, 1), F(T1, 0, 1), OP.is_le, deps=[pz, tc])
         y = scan(F(R6, 0, 96), C(cKeep, 0, 96), F(R5, 0, 96), OP.mult, OP.add, 0.0, [y])
-        z = ts(F(L, 0, 1), F(P, 0, 1), F(A3, t, t + 1), OP.mult, C(cJ, 0, 1), OP.add, deps=[z])
-        for b in (1, 2, 3):
-            for a in range(4):
-                lms = act(F(LM, 6 * a, 6 * a + 6, 32 * b, 32 * b + 32), F(R6, 15, 96, 32 * a, 32 * a + 32, 16), AF.Copy, [y])
+        z = ts(F(L, 0, 1), F(PS if last else P, 0, 1), F(A3, t, t + 1), OP.mult, C(cJ, 0, 1), OP.add, deps=[z])
+        lms = [act(F(LM, 6 * a, 6 * a + 6, 0, 32), F(R6, 15, 96, 32 * a, 32 * a + 32, 16), AF.Copy, [y]) for a in (2, 3)]
         for a in range(2):
             lmv = cp(F(LM, 6 * a, 6 * a + 6, 0, 32), F(R6, 15, 96, 32 * a, 32 * a + 32, 16), [y])
         z = ts(F(B2, 0, 32), C(cMask, 0, 32), F(L, 0, 1), OP.min, deps=[z])
-        for a in range(2, 4):
-            lmv = cp(F(LM, 6 * a, 6 * a + 6, 0, 32), F(R6, 15, 96, 32 * a, 32 * a + 32, 16), [y])
+        if last:
+            SG, AM = new(3), new(3)
+            lp = act(T.landp[:, R * r:R * r + R], T.places[:, 0:R], AF.Copy, [("xp", 3 * ne), pl])
+            sg = act(F(SG, 0, 3), F(A3, 0, 3), AF.Copy, [z], scale=2.0, bias=-1.0)
+            sg = act(F(AM, 0, 3), F(A3, 0, 3), AF.Copy, scale=1.0, bias=-1.0)
         for a in range(4):
             x = tr(F(R3, 32 * a, 32 * a + 32, 0, 32), F(B2, 0, 32, 32 * a, 32 * a + 32), [z])
-        x = scan(F(R4, 0, 128, 0, 32), C(cKeep, 0, 128, 0, 32), F(R3, 0, 128, 0, 32), OP.mult, OP.add, 0.0, [x])
         for b in range(4):
-            lqs = act(F(LQ, 0, 8, 32 * b, 32 * b + 32), F(R4, 15, 128, 0, 32, 16), AF.Copy, [x])
-        lm = cp(om[:, :], F(LM, 0, 24), [lms, lmv])
+            lm = cp(om[32 * b:32 * b + 32, :], F(LM, 0, 24, 0, 32), [lmv] + lms)
+        x = scan(F(R4, 0, 128, 0, 32), C(cKeep, 0, 128, 0, 32), F(R3, 0, 128, 0, 32), OP.mult, OP.add, 0.0, [x])
         if not last:
             m2, ms2, c0 = T["m%d" % (t + 1)], T["ms%d" % (t + 1)], 128
         else:
             m2, ms2, c0 = T.m3, T.ms3, 0
-        mc = cp(m2[:, c0:c0 + M].bitcast(u32), m[:, :].bitcast(u32).indirect(om[:, 0:24]), [lm, nd] + mdeps)
         mp = act(ms2[:, c0:c0 + M], ms[:, :].indirect(om[:, 0:24]), AF.Copy, [lm, nd] + mdeps)
+        for b in range(4):
+            lq = cp(oq[32 * b:32 * b + 32, :], F(R4, 15, 128, 0, 32, 16), [x])
+        mc = cp(m2[:, c0:c0 + M].bitcast(u32), m[:, :].bitcast(u32).indirect(om[:, 0:24]), [lm, nd] + mdeps)
         mdeps = [mc, mp]
-        lq = cp(oq[:, :], F(LQ, 0, 8), [lqs])
         if last:
             need("y", mc, mp)
             g.sync.dma_start(T.oc[:, :], T.m3[:, :].bitcast(u8)).then_inc(sem.out, 16)
             for k in range(4):
                 g.sync.dma_start(T.osc[4 * k:4 * k + 4, :], T.ms3[32 * k:32 * k + 4, :]).then_inc(sem.out, 16)
-            SG, AM = new(3), new(3)
-            lp = act(T.landp[:, R * r:R * r + R], T.places[:, 0:R], AF.Copy, [("xp", 3 * ne), pl])
-            sg = act(F(SG, 0, 3), F(A3, 0, 3), AF.Copy, [z], scale=2.0, bias=-1.0)
-            sg = act(F(AM, 0, 3), F(A3, 0, 3), AF.Copy, scale=1.0, bias=-1.0)
+            G12, G3, W1, WO = new(12), new(3), new(3), new(3)
+            x = tt(F(G12, 0, 12), F(OH, 0, 12), T.landp[:, :], OP.mult, [oh, lp, ("xp", 3 * ne)])
+            for c in range(3):
+                w = red(F(G3, c, c + 1), F(G12, c, 12, st=3), OP.add, [x])
         q2, qs2 = T["q%d" % (t + 1)], T["qs%d" % (t + 1)]
         ready = [lq, (x2, 2 * 3 * ne), ("own%d" % t, 32)] + qdeps
         qdeps = [cp(q2[:, 0:128].bitcast(u32), q[:, :].bitcast(u32).indirect(oq[:, 0:8]), ready),
                  act(qs2[:, 0:128], qs[:, :].indirect(oq[:, 0:8]), AF.Copy, ready)]
     y = mm(T.py[:, 0:128], T.wq[:, :], T.ws[:, :], T.q3[:, :], T.qs3[:, :], True, True, [kw] + qdeps)
-    G12, G3, W1, WO = new(12), new(3), new(3), new(3)
-    x = tt(F(G12, 0, 12), F(OH, 0, 12), T.landp[:, :], OP.mult, [oh, lp, ("xp", 3 * ne)])
-    for c in range(3):
-        w = red(F(G3, c, c + 1), F(G12, c, 12, st=3), OP.add, [x])
-    y = cp(T.yo[:, :], T.py[:, 0:128], [y])
     x = tt(F(W1, 0, 3), F(G3, 0, 3), F(SG, 0, 3), OP.mult, [w, sg])
     x = tt(F(WO, 0, 3), F(W1, 0, 3), F(AM, 0, 3), OP.add, [x])
-    need("y", y)
-    g.sync.dma_start(T.y[:, :], T.yo[:, :]).then_inc(sem.out, 16)
-    need("s", x)
+    y = act(T.yo[:, :], T.py[:, 0:128], AF.Copy, [y])
+    need("y", x)
     for c in range(R):
-        S.dma_start(T.wi[c:c + 1, :], F(WO, c, c + 1)).then_inc(sem.out, 16)
+        g.sync.dma_start(T.wi[c:c + 1, :], F(WO, c, c + 1)).then_inc(sem.out, 16)
+    need("s", y)
+    S.dma_start(T.y[:, :], T.yo[:, :]).then_inc(sem.out, 16)
     need("y", ("out", 16 * (1 + 4 + R + 1)))
     need("g", ("loc", local[0]), *[("c" + k, n) for k, n in count.items()])

from concourse.bass import DstId, RemoteDMATransfer
from concourse.mybir import dt, AluOpType, ActivationFunctionType, AxisListType

M, A, E, R = 384, 32, 40, 3
HM = M // 2
SL = 48
QW, QL = 128 + 4 * SL, 128 + 4 * 128
FW = 14000
CODE, U8, F32, BF, I32, U16 = "float8_e4m3fn_x4", "uint8", "float32", "bfloat16", "int32", "uint16"

SCRATCH = {
    "xt": ("sbuf", [128, 512], BF), "xq": ("sbuf", [128, 128], CODE), "xs": ("sbuf", [128, 128], U8),
    "met": ("sbuf", [128, 4 * M], BF),
    "wt": ("sbuf", [128, 512], BF), "wq": ("sbuf", [128, 128], CODE), "ws": ("sbuf", [128, 128], U8),
    "ce": ("sbuf", [128, 520 + 1024], F32), "et": ("sbuf", [128, 2048], BF), "eq": ("sbuf", [128, 512], CODE), "es": ("sbuf", [128, 512], U8),
    "ints": ("sbuf", [128, 64], I32),
    "cf": ("sbuf", [128, 1100], F32),
    "ff": ("sbuf", [128, FW], F32),
    "offx": ("sbuf", [128, 2], U16),
    "places": ("sbuf", [128, 4], F32), "landp": ("sbuf", [128, 12], F32),
    "yo": ("sbuf", [128, 128], F32),
    "m3": ("sbuf", [128, M], CODE), "ms3": ("sbuf", [128, M], U8),
    "q3": ("sbuf", [128, 128], CODE), "qs3": ("sbuf", [128, 128], U8),
    "pscore": ("psum", [128, 1024], F32), "pblend": ("psum", [128, 2048], F32), "py": ("psum", [128, 512], F32),
}
SEMAPHORES = ["cv", "cs", "ct", "cg", "lx", "lm", "lw", "x0", "xp", "loc", "out"]
for _t in range(R):
    _w = QL if _t == R - 1 else QW
    SCRATCH.update({
        "m%d" % _t: ("sbuf", [128, 128 + M], CODE), "ms%d" % _t: ("sbuf", [128, 128 + M], U8),
        "q%d" % _t: ("sbuf", [128, _w], CODE), "qs%d" % _t: ("sbuf", [128, _w], U8),
        "p%d" % _t: ("sbuf", [128, 128], CODE), "ps%d" % _t: ("sbuf", [128, 128], U8),
        "s%d" % _t: ("sbuf", [128, SL], CODE), "ss%d" % _t: ("sbuf", [128, SL], U8),
        "h%d" % _t: ("sbuf", [128, 512], BF),
        "land%d" % _t: ("sbuf", [128, 8], F32),
        "oc%d" % _t: ("sbuf", [128, 8], U16), "og%d" % _t: ("sbuf", [128, 4], U16),
        "oq%d" % _t: ("sbuf", [128, 8], U16), "om%d" % _t: ("sbuf", [128, 24], U16),
    })
    SEMAPHORES += ["x1_%d" % _t, "x2_%d" % _t, "own%d" % _t]


def rank_program(g, core, T, topo):
    r = T.rank_of(core)
    if r is None:
        return
    AF, OP, AXIS = ActivationFunctionType, AluOpType, AxisListType.X
    V, S, TE = g.vector, g.scalar, g.tensor
    others = [(r + k) % 4 for k in (1, 2, 3)]
    queue = {"v": V, "s": S, "t": TE, "g": g, "y": g.sync}
    count = {"v": 0, "s": 0, "t": 0, "g": 0}
    seen = {k: {} for k in queue}
    sem = T.sem

    def need(q, *deps):
        want = {}
        for d in deps:
            if d is not None:
                want[d[0]] = max(want.get(d[0], 0), d[1])
        for n, v in want.items():
            if seen[q].get(n, 0) < v:
                queue[q].wait_ge(sem[n], v)
                seen[q][n] = v

    def did(q, ins):
        count[q] += 1
        ins.then_inc(sem["c" + q], 1)
        return ("c" + q, count[q])

    def ts(out, in0, s1, op0, s2=None, op1=None, deps=()):
        need("v", *deps)
        if op1 is None:
            return did("v", V.tensor_scalar(out, in0, s1, None, op0))
        return did("v", V.tensor_scalar(out, in0, s1, s2, op0, op1))

    def tt(out, a, b, op, deps=()):
        need("v", *deps)
        return did("v", V.tensor_tensor(out, a, b, op))

    def red(out, a, op, deps=()):
        need("v", *deps)
        return did("v", V.tensor_reduce(out, a, AXIS, op))

    def scan(out, a, b, op0, op1, init, deps=()):
        need("v", *deps)
        return did("v", V.tensor_tensor_scan(out, a, b, init, op0, op1))

    def tr(out, a, deps=()):
        need("v", *deps)
        return did("v", V.transpose(out, a))

    def cp(out, a, deps=()):
        need("v", *deps)
        return did("v", V.tensor_copy(out, a))

    def fill(ap, c):
        return did("v", V.memset(ap, c))

    def qmx(o, s, i, deps=()):
        need("v", *deps)
        return did("v", V.quantize_mx(o, s, i))

    def act(out, a, func, deps=(), **k):
        need("s", *deps)
        return did("s", S.activation(out, a, func, **k))

    def mm(out, l, ls, x, xs, start, stop, deps=()):
        need("t", *deps)
        return did("t", TE.matmul_mx(out, l, ls, x, xs, start, stop))

    def io(*a, **k):
        return did("g", g.iota(*a, **k))

    used, cpos = [0], [0]

    def new(n):
        o = used[0]
        used[0] = o + (n + 7) // 8 * 8
        assert used[0] <= FW
        return o

    def F(o, c0, c1, p0=0, p1=128, st=1):
        return T.ff[p0:p1, o + c0:o + c1:st]

    def cnew(n):
        o = cpos[0]
        cpos[0] = o + (n + 7) // 8 * 8
        return o

    def C(o, c0, c1, p0=0, p1=128, st=1):
        return T.cf[p0:p1, o + c0:o + c1:st]

    local = [0]

    def send(src, dsts, rsem, deps):
        need("g", *deps)
        mask = topo.mask(core, T.cores[others[0]])
        ids = []
        for s in others:
            rid, pid, _ = topo.addr(T.cores[s])
            mask &= topo.mask(core, T.cores[s])
            ids.append(DstId(rid=rid, pnc=pid))
        g.remote_dma_fused([RemoteDMATransfer(dst_ids=ids, dma_engine_mask=mask, remote_sem=sem[rsem], srcs=[src], dsts=dsts)],
                           local_sem=sem["loc"])
        local[0] += bin(mask).count("1")

    u8, u32 = dt.uint8, dt.uint32
    ne = len(topo.engines(core, T.cores[others[0]]))

    g.sync.dma_start(T.xt[:, 0:4 * A], T.x[:, :]).then_inc(sem.lx, 16)
    S.dma_start(T.met[:, 0:2 * M], T.me[:, 0:2 * M]).then_inc(sem.lm, 16)
    g.sync.dma_start(T.met[:, 2 * M:4 * M], T.me[:, 2 * M:4 * M]).then_inc(sem.lm, 16)
    g.sync.dma_start(T.wt[:, :], T.w[:, :]).then_inc(sem.lw, 16)

    small = {"allow_small_or_imprecise_dtypes": True}
    cRow, cFour = cnew(32), cnew(4)
    cNeg, cKeep, cE, cZero, c2k = cnew(HM), cnew(128), cnew(128), cnew(32), cnew(32)
    cJ, cM16, cKb, cKc, cT0, cT1, cPl, cNp, cP31, cB = [cnew(n) for n in (1, 1, 3, 1, 1, 1, 3, 3, 1, 1)]
    cMask, cTri, cNm = cnew(32), cnew(32), cnew(32)
    i0 = io(T.ints[:, 0:1], [[0, 1]], 0, 1)
    i5 = io(T.ce[:, 0:512], [[1, 512]], 0, 0, **small)
    i4 = io(T.ce[:, 512:516], [[1, 4]], 0, 4, **small)
    z0 = fill(T.xt[:, 4 * A:512], 0.0)
    b0 = ts(T.ints[:, 1:2], T.ints[:, 0:1], 15, OP.bitwise_and, deps=[i0])
    a0 = cp(C(cJ, 0, 1), T.ints[:, 0:1])
    b1 = ts(T.ints[:, 2:3], T.ints[:, 0:1], 31, OP.bitwise_and)
    b2 = ts(T.ints[:, 3:4], T.ints[:, 0:1], 5, OP.arith_shift_right)
    a1 = cp(C(cM16, 0, 1), T.ints[:, 1:2], [b0])
    for c in range(3):
        kKb = ts(C(cKb, c, c + 1), C(cM16, 0, 1), 16.0 * c + 0.5, OP.add, deps=[a1])
    kOx = ts(T.offx[:, 0:2], C(cKb, 0, 2), -0.5, OP.add, deps=[kKb])
    qx = qmx(T.xq[:, :], T.xs[:, :], T.xt[:, :], [("lx", 16), z0])
    o0, o1 = A * r, A * r + A
    send(T.xq[:, 0:A].bitcast(u8), [T.q0[:, o0:o1].bitcast(u8)] * 3, "x0", [qx])
    send(T.xs[:, 0:A], [T.qs0[:, o0:o1]] * 3, "x0", [qx])
    i1 = io(T.ints[:, 16:48], [[1, 32]], 128, -1)
    i2 = io(C(cRow, 0, 32), [[1, 32]], 0, 0, **small)
    i3 = io(C(cFour, 0, 4), [[1, 4]], 1, 0, **small)
    own = cp(T.q0[:, o0:o1].bitcast(u32), T.xq[:, :].bitcast(u32).indirect(T.offx[:, 0:2]), [kOx, qx])
    owns = act(T.qs0[:, o0:o1], T.xs[:, :].indirect(T.offx[:, 0:2]), AF.Copy, [kOx, qx])
    ke = []
    for b in range(2):
        x = act(T.ce[:, 520 + 512 * b:1032 + 512 * b], T.ce[:, 0:512], AF.Abs, [i4, i5], scale=-1.0, bias=T.ce[:, 512 + b:513 + b])
        ke.append(act(T.et[:, 512 * b:512 * b + 512], T.ce[:, 520 + 512 * b:1032 + 512 * b], AF.Relu, [x], scale=-1.0, bias=0.5))
    a2 = cp(C(cP31, 0, 1), T.ints[:, 2:3], [b1])
    a3_ = ts(C(cB, 0, 1), T.ints[:, 3:4], 64.0, OP.mult, deps=[b2])
    f0 = fill(C(cNeg, 0, HM), -1e29)
    f1 = fill(C(cKeep, 0, 128), 1.0)
    f2 = fill(C(cE, 0, 128), float(E))
    f3 = fill(C(cZero, 0, 32), 0.0)
    memd = qmx(T.m0[:, 128:128 + M], T.ms0[:, 128:128 + M], T.met[:, :], [("lm", 32)])
    for b in (2, 3):
        ke.append(ts(T.et[:, 512 * b:512 * b + 512], T.ce[:, 0:512], T.ce[:, 512 + b:513 + b], OP.is_equal, 0.5, OP.mult, deps=[i4, i5]))
    f4 = fill(C(c2k, 0, 32), 2048.0)
    need("v", f1)
    f1 = fill(C(cKeep, 0, 128, st=16), 0.0)
    b3 = ts(T.ints[:, 16:48], T.ints[:, 16:48], 15, OP.bitwise_and, deps=[i1])
    kKc = ts(C(cKc, 0, 1), C(cJ, 0, 1), 2048.0, OP.add, deps=[a0])
    kT = ts(C(cT0, 0, 1), C(cJ, 0, 1), -1.0, OP.mult, float(127 - SL), OP.add)
    kT = ts(C(cT1, 0, 1), C(cJ, 0, 1), -1.0, OP.mult, float(127 - SL + E), OP.add)
    kmask = ts(C(cMask, 0, 32), T.ints[:, 16:48], 0.0, OP.is_equal, 1e6, OP.mult, deps=[b3])
    for h in range(3):
        kPl = ts(C(cPl, h, h + 1), C(cB, 0, 1), C(cJ, 0, 1), OP.add, 128.0 + 32 * h, OP.add, deps=[a3_])
    kTri = ts(C(cTri, 0, 32), C(cRow, 0, 32), C(cP31, 0, 1), OP.is_ge, 1e6, OP.mult, deps=[a2, i2])
    kNm = ts(C(cNm, 0, 32), C(cMask, 0, 32), float(HM) - 1e6, OP.add, deps=[kmask])
    kNp = ts(C(cNp, 0, 3), C(cPl, 0, 3), -127.0, OP.add, -2048.0, OP.mult, deps=[kPl])
    ke = qmx(T.eq[:, :], T.es[:, :], T.et[:, :], ke)
    WR, OH, A3, KF, K2, RW3 = new(128), new(12), new(3), new(136), new(136), new(16 * R)
    fWR = fill(F(WR, 0, 128), 0.0)
    fKF = fill(F(KF, 128, 136), 0.0)
    fK2 = fill(F(K2, 128, 136), -128.0)
    fRW = fill(F(RW3, 0, 16 * R), -1e29)
    kw = qmx(T.wq[:, :], T.ws[:, :], T.wt[:, :], [("lw", 16)])

    qdeps = [own, owns, ("x0", 2 * ne * 3)]
    mdeps = [memd]
    scan_prev, cast_prev = [None, None], []
    for t in range(R):
        land = T["land%d" % t]
        m, ms, q, qs = T["m%d" % t], T["ms%d" % t], T["q%d" % t], T["qs%d" % t]
        p, ps, s_, ss_ = T["p%d" % t], T["ps%d" % t], T["s%d" % t], T["ss%d" % t]
        h = T["h%d" % t]
        oc, og, oq, om = T["oc%d" % t], T["og%d" % t], T["oq%d" % t], T["om%d" % t]
        last = t == R - 1
        x1, x2 = "x1_%d" % t, "x2_%d" % t
        RM, JK, CN, C0, C1 = new(M), new(M), new(1), new(1), new(1)
        half = [F(RM, k, M, st=2) for k in range(2)]
        top = [F(RM, M - 2 + k, M - 1 + k) for k in range(2)]
        rm = []
        for k in range(2):
            rm.append(mm(T.pscore[:, 512 * k:512 * k + HM], q[:, 0:128], qs[:, 0:128], m[:, 128 + HM * k:128 + HM * k + HM],
                         ms[:, 128 + HM * k:128 + HM * k + HM], True, True, qdeps + mdeps + [scan_prev[k]]))
        rm = [scan(half[k], T.pscore[:, 512 * k:512 * k + HM], C(cNeg, 0, HM), OP.max, OP.max, -1e29, [rm[k], f0]) for k in range(2)]
        scan_prev = rm
        send(F(RM, M - 2, M), [land[:, 2 * r:2 * r + 2]] * 3, x1, rm)
        for b in range(4):
            dq = mm(T.pblend[:, 512 * b:512 * b + 128], T.eq[:, 128 * b:128 * b + 128], T.es[:, 128 * b:128 * b + 128],
                    q[:, 0:128], qs[:, 0:128], True, False, [ke] + cast_prev)
        B1, R1, R2, FC, K1, BA, NM, ME = new(32), new(128), new(128), new(1), new(1), new(1), new(32), new(1)
        c0_ = act(F(JK, 0, HM), half[0], AF.Sign, [rm[0]], scale=-1.0, bias=top[0], accum_out=F(C0, 0, 1))
        c1_ = act(F(JK, HM, M), half[1], AF.Sign, [rm[1]], scale=-1.0, bias=top[1], accum_out=F(C1, 0, 1))
        k1 = ts(F(K1, 0, 1), top[1], top[0], OP.is_le, 1e5, OP.mult, deps=rm)
        fc = ts(F(FC, 0, 1), top[1], top[0], OP.is_gt, 1e5, OP.mult)
        mx = tt(F(ME, 0, 1), top[0], top[1], OP.max)
        nm = ts(F(NM, 0, 32), C(cNm, 0, 32), F(K1, 0, 1), OP.add, deps=[k1, kNm])
        ba = ts(F(BA, 0, 1), F(FC, 0, 1), F(C0, 0, 1), OP.add, deps=[fc, c0_])
        bc = ts(F(B1, 0, 32), F(NM, 0, 32), F(C1, 0, 1), OP.add, F(BA, 0, 1), OP.min, deps=[nm, ba, c1_])
        for a in range(4):
            x = tr(F(R1, 32 * a, 32 * a + 32, 0, 32), F(B1, 0, 32, 32 * a, 32 * a + 32), [bc])
        k1 = ts(F(K1, 0, 1), F(K1, 0, 1), float(HM), OP.add)
        x = scan(F(R2, 0, 128, 0, 32), C(cKeep, 0, 128, 0, 32), F(R1, 0, 128, 0, 32), OP.mult, OP.max, 0.0, [x, f1])
        cn = ts(F(CN, 0, 1), F(C1, 0, 1), F(K1, 0, 1), OP.add, F(BA, 0, 1), OP.min, deps=[k1])
        for a in range(4):
            lc = cp(oc[32 * a:32 * a + 32, 0:8], F(R2, 15, 128, 0, 32, 16), [x])
        OW, KB = new(32), new(32)
        ow = act(F(OW, 0, 32), C(cZero, 0, 32), AF.Identity, [f3, mx], bias=F(ME, 0, 1))
        kb = act(F(KB, 0, 32), C(c2k, 0, 32), AF.Identity, [f4, cn, kKc], scale=F(CN, 0, 1), bias=C(cKc, 0, 1))
        pl = act(T.places[:, t:t + 1], F(CN, 0, 1), AF.Copy, [cn], bias=float(M * r))
        if last:
            send(T.places[:, 0:R], [T.landp[:, R * r:R * r + R]] * 3, "xp", [pl])
        pkc = cp(p[:, :].bitcast(u32), m[:, 128:128 + M].bitcast(u32).indirect(oc[:, 0:8]), [lc] + mdeps)
        pks = act(ps[:, :], ms[:, 128:128 + M].indirect(oc[:, 0:8]), AF.Copy, [lc] + mdeps)
        for a in range(4):
            kf = tr(F(KF, 32 * a, 32 * a + 32, 0, 32), F(KB, 0, 32, 32 * a, 32 * a + 32), [kb])
        bl = []
        for b in range(4):
            bl.append(mm(T.pblend[:, 512 * b:512 * b + 128], T.eq[:, 128 * b:128 * b + 128], T.es[:, 128 * b:128 * b + 128],
                         p[:, :], ps[:, :], False, True, [pkc, pks]))
        cast_prev = []
        for b in (0, 2):
            cast_prev.append(act(h[:, b:512:4], T.pblend[:, 512 * b:512 * b + 128], AF.Copy, [bl[b]]))
            cast_prev.append(cp(h[:, b + 1:512:4], T.pblend[:, 512 * b + 512:512 * b + 640], [bl[b + 1]]))
        for b in (1, 2, 3):
            kk = act(F(KF, 0, 128, 32 * b, 32 * b + 32), F(KF, 0, 128, 0, 32), AF.Copy, [kf])
        nd = qmx(m[:, 0:128], ms[:, 0:128], h[:, :], cast_prev)
        if last:
            k0 = 128 + 128 * r
            send(m[:, 0:128].bitcast(u8), [q[:, k0:k0 + 128].bitcast(u8)] * 3, x2, [nd])
            send(ms[:, 0:128], [qs[:, k0:k0 + 128]] * 3, x2, [nd])
            need("y", nd)
            g.sync.dma_start(q[:, k0:k0 + 128].bitcast(u8), m[:, 0:128].bitcast(u8)).then_inc(sem["own%d" % t], 16)
            g.sync.dma_start(qs[:, k0:k0 + 128], ms[:, 0:128]).then_inc(sem["own%d" % t], 16)
        x1 = (x1, 3 * ne)
        MX, FL, MI, MR, AC, CS = new(1), new(1), new(32), new(128), new(3), new(128)
        RW, S1, J3, BW, BT = RW3 + 16 * t, new(1), new(5), new(32), new(32)
        lo = act(land[:, 2 * r:2 * r + 2], F(RM, M - 2, M), AF.Copy, [x1])
        if r == 0:
            x = red(F(MX, 0, 1), land[:, 2:8], OP.max, [x1])
            mi = ts(F(MI, 0, 32), F(OW, 0, 32), F(MX, 0, 1), OP.is_ge, deps=[x, ow])
        elif r == 3:
            x = red(F(MX, 0, 1), land[:, 0:6], OP.max, [x1])
            mi = ts(F(MI, 0, 32), F(OW, 0, 32), F(MX, 0, 1), OP.is_gt, deps=[x, ow])
        elif r == 1:
            x = red(F(MX, 0, 1), land[:, 4:8], OP.max, [x1])
            x = ts(F(FL, 0, 1), land[:, 0:1], land[:, 1:2], OP.max, F(ME, 0, 1), OP.is_lt, deps=[mx])
            mi = ts(F(MI, 0, 32), F(OW, 0, 32), F(MX, 0, 1), OP.is_ge, F(FL, 0, 1), OP.mult, deps=[x, ow])
        else:
            x = red(F(MX, 0, 1), land[:, 0:4], OP.max, [x1])
            x = ts(F(FL, 0, 1), land[:, 6:7], land[:, 7:8], OP.max, F(ME, 0, 1), OP.is_le, deps=[mx])
            mi = ts(F(MI, 0, 32), F(OW, 0, 32), F(MX, 0, 1), OP.is_gt, F(FL, 0, 1), OP.mult, deps=[x, ow])
        for a in range(4):
            x = tr(F(MR, 32 * a, 32 * a + 32, 0, 32), F(MI, 0, 32, 32 * a, 32 * a + 32), [mi])
        cs = scan(F(CS, 0, 128, 0, 32), F(MR, 0, 128, 0, 32), C(cE, 0, 128, 0, 32), OP.add, OP.min, 0.0, [x, f2])
        for c in range(2):
            ac = act(F(new(128), 0, 128, 0, 32), F(CS, 0, 128, 0, 32), AF.Sign, [cs, kKb], scale=-1.0, bias=C(cKb, c, c + 1, 0, 32),
                     accum_out=F(AC, c, c + 1, 0, 32))
        x = ts(F(K2, 0, 128, 0, 32), F(CS, 0, 128, 0, 32), C(cKb, 2, 3, 0, 32), OP.is_le, 2.0, OP.mult, deps=[cs, kKb])
        rw = scan(F(RW, 1, 9), land[:, 0:8], C(cNeg, 0, 8), OP.max, OP.max, -1e29, [lo, x1, fRW])
        av = red(F(AC, 2, 3, 0, 32), F(K2, 0, 129, 0, 32), OP.add, [x, fK2])
        EQ, T1 = new(136), new(1)
        s1 = act(F(J3, 0, 5), F(RW, 0, 9, st=2), AF.Sign, [rw], scale=-1.0, bias=F(RW, 8, 9), accum_out=F(S1, 0, 1))
        bw = act(F(BW, 0, 32), C(cZero, 0, 32), AF.Identity, [s1], bias=F(S1, 0, 1))
        for a in range(4):
            lg = ts(og[32 * a:32 * a + 32, 0:3], F(AC, 0, 3, 0, 32), 0.5, OP.mult, 64.0, OP.add, deps=[ac, av])
        if not last:
            gc = cp(s_[:, :].bitcast(u32), m[:, :].bitcast(u32).indirect(og[:, 0:3]), [lg, nd])
            gs = act(ss_[:, :], ms[:, :].indirect(og[:, 0:3]), AF.Copy, [lg, nd])
            k0 = 128 + SL * r
            send(s_[:, 0:E].bitcast(u8), [q[:, k0:k0 + E].bitcast(u8)] * 3, x2, [gc])
            send(ss_[:, 0:E], [qs[:, k0:k0 + E]] * 3, x2, [gs])
            need("y", gc, gs)
            g.sync.dma_start(q[:, k0:k0 + SL].bitcast(u8), s_[:, :].bitcast(u8)).then_inc(sem["own%d" % t], 16)
            g.sync.dma_start(qs[:, k0:k0 + SL], ss_[:, :]).then_inc(sem["own%d" % t], 16)
        KG, AB, P, L, B2, R3, R4 = new(SL), new(3 * SL), new(1), new(1), new(32), new(128), new(128)
        D, BM, R5, R6, LM, PS = new(3), new(96), new(96), new(96), new(24), new(1)
        kg = act(F(KG, 0, SL), F(KF, 0, 136).indirect(og[:, 0:3]), AF.Copy, [kk, fKF, lg])
        ab = [act(F(AB, SL * c, SL * c + SL), F(KG, 0, SL), AF.Abs, [kg, kNp], bias=C(cNp, c, c + 1)) for c in range(3)]
        tc = act(F(EQ, 128, 129), F(S1, 0, 1), AF.Identity, [kT, s1], scale=float(SL), bias=C(cT0, 0, 1))
        tc = act(F(T1, 0, 1), F(S1, 0, 1), AF.Identity, scale=float(SL), bias=C(cT1, 0, 1))
        if last:
            tc = act(F(PS, 0, 1), F(S1, 0, 1), AF.Copy, scale=128.0)
        bt = ts(F(BT, 0, 32), C(cTri, 0, 32), F(S1, 0, 1), OP.min, deps=[s1, kTri])
        for b in range(1, 4):
            for a in range(b):
                x = tr(F(WR, 32 + 32 * a, 64 + 32 * a, 32 * b, 32 * b + 32), F(BW, 0, 32, 32 * a, 32 * a + 32), [bw, fWR])
        x = tr(F(WR, 0, 32), F(BT, 0, 32), [bt])
        d = [red(F(D, c, c + 1), F(AB, SL * c, SL * c + SL), OP.min, [ab[c]]) for c in range(3)]
        eq = ts(F(EQ, 0, 128), F(WR, 0, 128), F(S1, 0, 1), OP.is_equal, deps=[x])
        pz = act(F(new(136), 0, 129), F(EQ, 0, 129), AF.Copy, [eq, tc], accum_out=F(P, 0, 1))
        for c in range(3):
            bm = ts(F(BM, 32 * c, 32 * c + 32), C(cMask, 0, 32), F(D, c, c + 1), OP.min, C(cPl, c, c + 1), OP.min, deps=[d[c]])
        oh = ts(F(OH, t, 12, st=3), C(cFour, 0, 4), F(S1, 0, 1), OP.is_equal, deps=[i3])
        y = tr(F(R5, 0, 96), F(BM, 0, 96), [bm])
        z = ts(F(A3, t, t + 1), F(P, 0, 1), F(T1, 0, 1), OP.is_le, deps=[pz, tc])
        y = scan(F(R6, 0, 96), C(cKeep, 0, 96), F(R5, 0, 96), OP.mult, OP.add, 0.0, [y])
        z = ts(F(L, 0, 1), F(PS if last else P, 0, 1), F(A3, t, t + 1), OP.mult, C(cJ, 0, 1), OP.add, deps=[z])
        lms = [act(F(LM, 6 * a, 6 * a + 6, 0, 32), F(R6, 15, 96, 32 * a, 32 * a + 32, 16), AF.Copy, [y]) for a in (2, 3)]
        for a in range(2):
            lmv = cp(F(LM, 6 * a, 6 * a + 6, 0, 32), F(R6, 15, 96, 32 * a, 32 * a + 32, 16), [y])
        z = ts(F(B2, 0, 32), C(cMask, 0, 32), F(L, 0, 1), OP.min, deps=[z])
        if last:
            SG, AM = new(3), new(3)
            lp = act(T.landp[:, R * r:R * r + R], T.places[:, 0:R], AF.Copy, [("xp", 3 * ne), pl])
            sg = act(F(SG, 0, 3), F(A3, 0, 3), AF.Copy, [z], scale=2.0, bias=-1.0)
            sg = act(F(AM, 0, 3), F(A3, 0, 3), AF.Copy, scale=1.0, bias=-1.0)
        for a in range(4):
            x = tr(F(R3, 32 * a, 32 * a + 32, 0, 32), F(B2, 0, 32, 32 * a, 32 * a + 32), [z])
        for b in range(4):
            lm = cp(om[32 * b:32 * b + 32, :], F(LM, 0, 24, 0, 32), [lmv] + lms)
        x = scan(F(R4, 0, 128, 0, 32), C(cKeep, 0, 128, 0, 32), F(R3, 0, 128, 0, 32), OP.mult, OP.add, 0.0, [x])
        if not last:
            m2, ms2, c0 = T["m%d" % (t + 1)], T["ms%d" % (t + 1)], 128
        else:
            m2, ms2, c0 = T.m3, T.ms3, 0
        mp = act(ms2[:, c0:c0 + M], ms[:, :].indirect(om[:, 0:24]), AF.Copy, [lm, nd] + mdeps)
        for b in range(4):
            lq = cp(oq[32 * b:32 * b + 32, :], F(R4, 15, 128, 0, 32, 16), [x])
        mc = cp(m2[:, c0:c0 + M].bitcast(u32), m[:, :].bitcast(u32).indirect(om[:, 0:24]), [lm, nd] + mdeps)
        mdeps = [mc, mp]
        if last:
            need("y", mc, mp)
            g.sync.dma_start(T.oc[:, :], T.m3[:, :].bitcast(u8)).then_inc(sem.out, 16)
            for k in range(4):
                g.sync.dma_start(T.osc[4 * k:4 * k + 4, :], T.ms3[32 * k:32 * k + 4, :]).then_inc(sem.out, 16)
            G12, G3, W1, WO = new(12), new(3), new(3), new(3)
            x = tt(F(G12, 0, 12), F(OH, 0, 12), T.landp[:, :], OP.mult, [oh, lp, ("xp", 3 * ne)])
            for c in range(3):
                w = red(F(G3, c, c + 1), F(G12, c, 12, st=3), OP.add, [x])
        q2, qs2 = T["q%d" % (t + 1)], T["qs%d" % (t + 1)]
        ready = [lq, (x2, 2 * 3 * ne), ("own%d" % t, 32)] + qdeps
        qdeps = [cp(q2[:, 0:128].bitcast(u32), q[:, :].bitcast(u32).indirect(oq[:, 0:8]), ready),
                 act(qs2[:, 0:128], qs[:, :].indirect(oq[:, 0:8]), AF.Copy, ready)]
    y = mm(T.py[:, 0:128], T.wq[:, :], T.ws[:, :], T.q3[:, :], T.qs3[:, :], True, True, [kw] + qdeps)
    x = tt(F(W1, 0, 3), F(G3, 0, 3), F(SG, 0, 3), OP.mult, [w, sg])
    x = tt(F(WO, 0, 3), F(W1, 0, 3), F(AM, 0, 3), OP.add, [x])
    y = act(T.yo[:, :], T.py[:, 0:128], AF.Copy, [y])
    need("y", x)
    for c in range(R):
        g.sync.dma_start(T.wi[c:c + 1, :], F(WO, c, c + 1)).then_inc(sem.out, 16)
    need("s", y)
    S.dma_start(T.y[:, :], T.yo[:, :]).then_inc(sem.out, 16)
    need("y", ("out", 16 * (1 + 4 + R + 1)))
    need("g", ("loc", local[0]), *[("c" + k, n) for k, n in count.items()])
